import numpy as np
import ml_dtypes


def mxq(x, axis, fmt="e4m3"):
    dtype, down = {"e4m3": (ml_dtypes.float8_e4m3fn, 7), "e5m2": (ml_dtypes.float8_e5m2, 14)}[fmt]
    v = np.moveaxis(np.asarray(x, np.float32).astype(ml_dtypes.bfloat16).astype(np.float64), axis, -1)
    blocks = v.reshape(v.shape[:-1] + (-1, 32))
    amax = np.abs(blocks).max(-1, keepdims=True)
    byte = np.maximum(np.where(amax > 0, np.frexp(amax)[1] - 1 + 127, 0) - down, 1)
    scale = np.exp2(byte - 127.0)
    codes = (blocks / scale).astype(np.float32).astype(dtype).astype(np.float64)
    return np.moveaxis((codes * scale).reshape(v.shape), -1, axis)


WIDE = False


def mx_kscale(k):
    if not WIDE:
        return np.ones(k)
    levels = np.array([24, -24, 12, -12, 0])
    if k % 512:
        return np.exp2(np.random.permutation(np.resize(levels, k // 32))).repeat(32)
    a = np.empty((k // 512, 16))
    for p in range(k // 512):
        a[p, :8] = np.random.permutation(np.resize(levels, 8))
        for g in range(8):
            far = levels[np.abs(levels - a[p, g]) >= 10]
            a[p, g + 8] = far[np.random.randint(len(far))]
    return np.exp2(a.ravel()).repeat(32)


def f64(x):
    return np.asarray(x).astype(np.float64)


def striped(idx):
    return np.tile(idx.reshape(-1, 16).T, (8, 1)).astype(np.uint16)


def unstriped(offs):
    return offs[:16].T.reshape(-1).astype(np.int64)


E2M1 = np.array([0.0, 0.5, 1.0, 1.5, 2.0, 3.0, 4.0, 6.0, -0.0, -0.5, -1.0, -1.5, -2.0, -3.0, -4.0, -6.0])


def pack_weight(w, fmt):
    k, n = w.shape
    w = f64(np.asarray(w, np.float32).astype(ml_dtypes.bfloat16)).reshape(k // 32, 32, n)
    amax = np.abs(w).max(1)
    if fmt == "e4m3":
        byte = np.frexp(amax)[1] - 1 + 127 - 7
    else:
        mant, ex = np.frexp(amax / 6.0)
        byte = np.where(mant > 0.5, ex, ex - 1) + 127
    byte = np.clip(np.where(amax > 0, byte, 1), 1, 254)
    scaled = (w * np.exp2(127.0 - byte)[:, None, :]).reshape(k, n).astype(np.float32)
    by_word = np.ascontiguousarray(scaled.reshape(k // 512, 128, 4, n).transpose(0, 1, 3, 2))
    if fmt == "e4m3":
        words = by_word.astype(ml_dtypes.float8_e4m3fn).view(np.uint8)
    else:
        c = by_word.astype(ml_dtypes.float4_e2m1fn).view(np.uint8) & 0xF
        words = (c[..., 0::2] | (c[..., 1::2] << 4)).reshape(k // 512, 128, 2 * n)
    return np.ascontiguousarray(words), np.ascontiguousarray(byte.astype(np.uint8).reshape(k // 512, 16, n))


def unpack_weight(words, scales, fmt):
    g, _, n = scales.shape
    words = np.ascontiguousarray(words).reshape(g, 128, n, -1)
    if fmt == "e4m3":
        vals = words.view(ml_dtypes.float8_e4m3fn).astype(np.float64)
    else:
        nib = np.empty((g, 128, n, 4), np.uint8)
        nib[..., 0::2] = words & 0xF
        nib[..., 1::2] = words >> 4
        vals = E2M1[nib]
    vals = vals * np.repeat(np.exp2(scales.astype(np.float64) - 127.0), 8, axis=1)[..., None]
    return vals.transpose(0, 1, 3, 2).reshape(g * 512, n)


def pack_table4(v):
    words, scales = pack_weight(v, "e2m1")
    g, t = words.shape[0] // 2, v.shape[1]
    return np.ascontiguousarray(words.reshape(g, 2, 128, t, 2).transpose(0, 2, 3, 1, 4).reshape(g, 128, t, 4)), scales


def unpack_table4(words, scales):
    g, _, t, _ = words.shape
    return unpack_weight(words.reshape(g, 128, t, 2, 2).transpose(0, 3, 1, 2, 4).reshape(2 * g, 128, 2 * t), scales, "e2m1")


def sigm(f):
    return 1.0 / (1.0 + np.exp(-np.maximum(f, -700.0)))


K, L, N, T, J = 1024, 512, 512, 2048, 1024


def setup_inputs():
    n = np.random.standard_normal
    s = mx_kscale(K)[:, None]
    s2 = mx_kscale(L)[:, None]
    p_tab = pack_table4(n((K, T)) * s)
    p_tab2 = pack_weight(n((L, T)) * s2, "e4m3")
    p_zv = pack_weight(n((K, N)) / np.sqrt(K) / s, "e4m3")
    p_zt = pack_weight(n((L, N)) / np.sqrt(L) / s2, "e2m1")
    p_wt = pack_weight(n((L, N)) / np.sqrt(L) / s2, "e2m1")
    return {
        "tab_words": p_tab[0],
        "tab_scales": p_tab[1],
        "tab2_words": p_tab2[0],
        "tab2_scales": p_tab2[1],
        "zv_words": p_zv[0],
        "zv_scales": p_zv[1],
        "zt_words": p_zt[0],
        "zt_scales": p_zt[1],
        "b": (0.3 * n(N)).astype(np.float32),
        "wv": (n((K, N)) / np.sqrt(K) / s).astype(np.float32),
        "wt_words": p_wt[0],
        "wt_scales": p_wt[1],
        "offs": striped(np.random.permutation(T)[:J]),
        "offs2": striped(np.random.permutation(T)[:J]),
    }


def reference(tab_words, tab_scales, tab2_words, tab2_scales, zv_words, zv_scales, zt_words, zt_scales, b, wv, wt_words, wt_scales, offs, offs2):
    idx = unstriped(offs)
    idx2 = unstriped(offs2)
    tab_ = unpack_table4(tab_words, tab_scales)[:, idx]
    tab2_ = unpack_weight(tab2_words, tab2_scales, "e4m3")[:, idx2]
    zv_ = unpack_weight(zv_words, zv_scales, "e4m3")
    zt_ = unpack_weight(zt_words, zt_scales, "e2m1")
    z = zv_.T @ tab_ + zt_.T @ tab2_
    gate = sigm(z + f64(b)[:, None])
    wv_ = mxq(f64(wv), 0, "e4m3")
    wt_ = unpack_weight(wt_words, wt_scales, "e2m1")
    hv = wv_.T @ tab_
    ht = wt_.T @ tab2_
    av = np.tanh(hv)
    at = np.tanh(ht)
    return at + gate * (av - at)

@@ -1,0 +1,239 @@
+from contextlib import ExitStack
+
+import concourse.mybir as mybir
+
+K, L, N, T, J = 1024, 512, 512, 2048, 1024
+FLOPS = 2 * J * N * (2 * K + 2 * L)
+
+F32 = mybir.dt.float32
+BF16 = mybir.dt.bfloat16
+I32 = mybir.dt.int32
+U32 = mybir.dt.uint32
+U16 = mybir.dt.uint16
+U8 = mybir.dt.uint8
+FP8X4 = mybir.dt.float8_e4m3fn_x4
+FP4X4 = mybir.dt.float4_e2m1fn_x4
+TANH = mybir.ActivationFunctionType.Tanh
+ADD, SUB, MULT = mybir.AluOpType.add, mybir.AluOpType.subtract, mybir.AluOpType.mult
+
+P = 128
+PACK = 4
+K_PASS = P * PACK
+K_PASSES = K // K_PASS
+QUADS, QUAD, ROWS = 4, 32, 4
+TOP = QUAD - K_PASSES * ROWS
+SPAN = QUAD * (QUADS - 1) + ROWS
+HALF = 512
+EARLY = 6
+RING = 4
+HALVES = J // HALF
+LIST_COLS = HALF // 16
+WV_COLS = 256
+WV_PARTS = N // WV_COLS
+CHUNKS = WV_COLS // P
+
+
+def tile_list_gmu_tanh_none_kernel(
+    tc, tab_words, tab_scales, tab2_words, tab2_scales, zv_words, zv_scales, zt_words, zt_scales,
+    b, wv, wt_words, wt_scales, offs, offs2, out,
+):
+    nc = tc.nc
+    with ExitStack() as ctx:
+        keep = ctx.enter_context(tc.tile_pool(name="keep", bufs=1))
+        work = ctx.enter_context(tc.tile_pool(name="work", bufs=8))
+        psum = ctx.enter_context(tc.psum_pool(name="psum", bufs=1))
+
+        def held(shape, dtype, name):
+            return keep.tile(shape, dtype, name=name, align_bytes=64)
+
+        list1 = held([P, J // 16], U16, "list1")
+        list2 = held([P, J // 16], U16, "list2")
+        tab_s = held([P, T], U8, "tab_s")
+        tab2_s = held([P, T], U8, "tab2_s")
+        tab_w = held([P, T], U32, "tab_w")
+        tab2_w = held([P, T], U32, "tab2_w")
+        zv_w = held([P, K_PASSES, N], U32, "zv_w")
+        zv_s = held([P, K_PASSES, N], U8, "zv_s")
+        zt_w = held([P, 2 * N], U8, "zt_w")
+        zt_s = held([P, N], U8, "zt_s")
+        wt_w = held([P, 2 * N], U8, "wt_w")
+        wt_s = held([P, N], U8, "wt_s")
+        bias = held([P, N // P], F32, "bias")
+        half_bias = held([P, N // P], F32, "half_bias")
+        v_top = held([P, J], U8, "v_top")
+        v_s = held([P, K_PASSES, J], U8, "v_s")
+        v2_s = held([P, J], U8, "v2_s")
+        wv_raw = [[held([P, PACK, WV_COLS], F32, "wv_raw%d%d" % (g, a)) for a in range(K_PASSES)] for g in range(WV_PARTS)]
+        wv_bf = [held([P, K_PASSES, WV_COLS, PACK], BF16, "wv_bf%d" % g) for g in range(WV_PARTS)]
+        wv_w = [held([P, K_PASSES * WV_COLS], U32, "wv_w%d" % g) for g in range(WV_PARTS)]
+        wv_s = [held([P, K_PASSES * WV_COLS], U8, "wv_s%d" % g) for g in range(WV_PARTS)]
+        v_w = [held([P, K_PASSES, 2 * HALF], U8, "v_w%d" % h) for h in range(HALVES)]
+        v2_w = [held([P, HALF], U32, "v2_w%d" % h) for h in range(HALVES)]
+        pairs = held([P, HALF], U32, "pairs")
+        banks = [psum.tile([P, HALF], F32, name="bank%d" % i) for i in range(2 * RING)]
+
+        for q in range(QUADS):
+            nc.vector.memset(tab_s[QUAD * q : QUAD * q + TOP, :].bitcast(I32), 0)
+        two_passes = "p a n -> p (a n)"
+        for plane in (tab2_s[:], wt_s[:], v_s[:].rearrange(two_passes), zv_s[:].rearrange(two_passes), zt_s[:]):
+            nc.gpsimd.memset(plane.bitcast(I32), 0)
+
+        def gather(dst, window, offsets):
+            nc.vector.tensor_copy(dst, window[:].indirect(offsets))
+
+        def load_plane(tile, scales):
+            for q in range(QUADS):
+                nc.sync.dma_start(
+                    out=tile[QUAD * q : QUAD * q + ROWS, :].bitcast(I32),
+                    in_=scales[0, ROWS * q : ROWS * (q + 1), :].bitcast(I32),
+                )
+
+        def load_wv(g, a):
+            rows = wv[a * K_PASS : (a + 1) * K_PASS, g * WV_COLS : (g + 1) * WV_COLS]
+            nc.sync.dma_start(out=wv_raw[g][a][:], in_=rows.rearrange("(p j) n -> p j n", j=PACK))
+
+        def load_table(tile, words):
+            nc.sync.dma_start(out=tile[:].bitcast(I32), in_=words[0].rearrange("p t i -> p (t i)").bitcast(I32))
+
+        nc.sync.dma_start(list1[:], offs)
+        for q in range(QUADS):
+            nc.sync.dma_start(
+                out=tab_s[QUAD * q + TOP : QUAD * (q + 1), :].bitcast(I32),
+                in_=tab_scales[:, ROWS * q : ROWS * (q + 1), :].bitcast(I32),
+            )
+        load_wv(0, 0)
+        with nc.allow_non_contiguous_dma(reason="one bias value a partition"):
+            nc.sync.dma_start(out=bias[:], in_=b.rearrange("(c p) -> p c", p=P))
+        nc.sync.dma_start(list2[:], offs2)
+        load_plane(tab2_s, tab2_scales)
+        load_table(tab2_w, tab2_words)
+        load_wv(0, 1)
+        nc.sync.dma_start(out=wt_w[:].bitcast(I32), in_=wt_words[0].bitcast(I32))
+        load_plane(wt_s, wt_scales)
+        load_table(tab_w, tab_words)
+        gather(v_top[:], tab_s, list1[:])
+        for a in range(K_PASSES):
+            first = TOP + a * ROWS
+            nc.sync.dma_start(out=v_s[0:SPAN, a, :].bitcast(I32), in_=v_top[first : first + SPAN, :].bitcast(I32))
+        for q in range(QUADS):
+            nc.sync.dma_start(
+                out=zv_s[QUAD * q : QUAD * q + ROWS, :, :].bitcast(I32),
+                in_=zv_scales[:, ROWS * q : ROWS * (q + 1), :].rearrange("a r n -> r a n").bitcast(I32),
+            )
+        nc.sync.dma_start(out=zv_w[:].bitcast(I32), in_=zv_words.rearrange("a p n i -> p a (n i)").bitcast(I32))
+        nc.sync.dma_start(out=zt_w[:].bitcast(I32), in_=zt_words[0].bitcast(I32))
+        load_plane(zt_s, zt_scales)
+        load_wv(1, 0)
+        load_wv(1, 1)
+        nc.gpsimd.tensor_scalar(half_bias[:], bias[:], 0.5, 0.0, MULT, ADD)
+
+        def half_list(lst, h):
+            return lst[:, h * LIST_COLS : (h + 1) * LIST_COLS]
+
+        def round_wv(g):
+            for a in range(K_PASSES):
+                nc.scalar.copy(
+                    out=wv_bf[g][:, a].rearrange("p (c i) t -> p c t i", i=PACK),
+                    in_=wv_raw[g][a][:].rearrange("p t (c i) -> p c t i", i=PACK),
+                )
+
+        def quantise_wv(g):
+            nc.vector.quantize_mx(
+                out=wv_w[g][:].bitcast(FP8X4), scales=wv_s[g][:], in_=wv_bf[g][:].rearrange("p a n t -> p (a n t)")
+            )
+
+        def part(h):
+            nc.vector.tensor_copy(
+                out=v_w[h][:].bitcast(U16), in_=pairs[:].bitcast(U16).rearrange("p (j d) -> p d j", d=K_PASSES)
+            )
+
+        gather(v2_s[:], tab2_s, list2[:])
+        for h in range(HALVES):
+            gather(v2_w[h][:], tab2_w, half_list(list2, h))
+        round_wv(0)
+        quantise_wv(0)
+        for h in range(HALVES):
+            gather(pairs[:], tab_w, half_list(list1, h))
+            part(h)
+
+        def text(h):
+            return dict(rhs=v2_w[h][:].bitcast(FP8X4), rhs_scale=v2_s[:, h * HALF : (h + 1) * HALF])
+
+        def picture(h, a):
+            return dict(rhs=v_w[h][:, a, :].bitcast(FP4X4), rhs_scale=v_s[:, a, h * HALF : (h + 1) * HALF])
+
+        def make_at(c, h, bank):
+            nc.tensor.matmul_mx(
+                out=bank[:], lhsT=wt_w[:, 2 * c * P : 2 * (c + 1) * P].bitcast(FP4X4), lhsT_scale=wt_s[:, c * P : (c + 1) * P],
+                start=True, stop=True, **text(h),
+            )
+            at = work.tile([P, HALF], F32, name="at")
+            nc.scalar.activation(at[:], bank[:], TANH)
+            return at
+
+        def make_tg(c, h, bank):
+            cols = slice(c * P, (c + 1) * P)
+            nc.tensor.matmul_mx(
+                out=bank[:], lhsT=zt_w[:, 2 * c * P : 2 * (c + 1) * P].bitcast(FP4X4), lhsT_scale=zt_s[:, cols],
+                start=True, stop=False, **text(h),
+            )
+            for a in range(K_PASSES):
+                nc.tensor.matmul_mx(
+                    out=bank[:], lhsT=zv_w[:, a, cols].bitcast(FP8X4), lhsT_scale=zv_s[:, a, cols],
+                    start=False, stop=(a == K_PASSES - 1), **picture(h, a),
+                )
+            tg = work.tile([P, HALF], F32, name="tg")
+            nc.scalar.activation(tg[:], bank[:], TANH, bias=half_bias[:, c : c + 1], scale=0.5)
+            return tg
+
+        def make_av(c, h, bank):
+            g, cc = divmod(c, CHUNKS)
+            for a in range(K_PASSES):
+                wcols = slice(a * WV_COLS + cc * P, a * WV_COLS + (cc + 1) * P)
+                nc.tensor.matmul_mx(
+                    out=bank[:], lhsT=wv_w[g][:, wcols].bitcast(FP8X4), lhsT_scale=wv_s[g][:, wcols],
+                    start=(a == 0), stop=(a == K_PASSES - 1), **picture(h, a),
+                )
+            av = work.tile([P, HALF], F32, name="av")
+            nc.scalar.activation(av[:], bank[:], TANH)
+            return av
+
+        tiles = [(c, h) for h in range(HALVES) for c in range(N // P)]
+        made = {}
+        for i, (c, h) in enumerate(tiles[:EARLY]):
+            made["at", c, h] = make_at(c, h, banks[RING + i % RING])
+
+        turns = []
+
+        def in_ring(kind, maker, c, h):
+            made[kind, c, h] = maker(c, h, banks[len(turns) % RING])
+            turns.append(kind)
+
+        def blend(g, h):
+            chunks = range(g * CHUNKS, (g + 1) * CHUNKS)
+            for c in chunks:
+                if ("at", c, h) not in made:
+                    in_ring("at", make_at, c, h)
+                if g == 0 and h == 0:
+                    in_ring("av", make_av, c, h)
+                    in_ring("tg", make_tg, c, h)
+                else:
+                    in_ring("tg", make_tg, c, h)
+                    in_ring("av", make_av, c, h)
+            diffs = [work.tile([P, HALF], F32, name="diff") for c in chunks]
+            gated = [work.tile([P, HALF], F32, name="gated") for c in chunks]
+            res = [work.tile([P, HALF], F32, name="res") for c in chunks]
+            for c, d in zip(chunks, diffs):
+                nc.vector.tensor_tensor(d[:], made["av", c, h][:], made["at", c, h][:], SUB)
+            for c, d, m in zip(chunks, diffs, gated):
+                nc.vector.scalar_tensor_tensor(m[:], made["tg", c, h][:], 1.0, d[:], ADD, MULT)
+            for c, m, r in zip(chunks, gated, res):
+                nc.vector.scalar_tensor_tensor(r[:], m[:], 0.5, made["at", c, h][:], MULT, ADD)
+                made["res", c, h] = r
+                nc.sync.dma_start(out=out[c * P : (c + 1) * P, h * HALF : (h + 1) * HALF], in_=r[:])
+
+        round_wv(1)
+        quantise_wv(1)
+        for g in range(WV_PARTS):
+            for h in range(HALVES):
+                blend(g, h)

@@ -24,7 +24,7 @@ QUADS, QUAD, ROWS = 4, 32, 4
 TOP = QUAD - K_PASSES * ROWS
 SPAN = QUAD * (QUADS - 1) + ROWS
 HALF = 512
-EARLY = 6
+EARLY = 7
 RING = 4
 HALVES = J // HALF
 LIST_COLS = HALF // 16
@@ -206,14 +206,15 @@ def tile_list_gmu_tanh_none_kernel(
         turns = []
 
         def in_ring(kind, maker, c, h):
-            made[kind, c, h] = maker(c, h, banks[len(turns) % RING])
+            pair, turn = divmod(len(turns), RING)
+            made[kind, c, h] = maker(c, h, banks[RING * (max(pair - 1, 0) % 2) + turn])
             turns.append(kind)
 
         def blend(g, h):
             chunks = range(g * CHUNKS, (g + 1) * CHUNKS)
             for c in chunks:
                 if ("at", c, h) not in made:
-                    in_ring("at", make_at, c, h)
+                    made["at", c, h] = make_at(c, h, banks[RING])
                 if g == 0 and h == 0:
                     in_ring("av", make_av, c, h)
                     in_ring("tg", make_tg, c, h)

@@ -21,11 +21,12 @@ PACK = 4
 K_PASS = P * PACK
 K_PASSES = K // K_PASS
 QUADS, QUAD, ROWS = 4, 32, 4
-TOP = QUAD - K_PASSES * ROWS
-SPAN = QUAD * (QUADS - 1) + ROWS
+BLOCKS = QUADS * ROWS
+LAST_QUAD = QUAD * (QUADS - 1)
 HALF = 512
-EARLY = 7
 RING = 4
+FIRST_MOVES = 4
+EARLY = 7
 HALVES = J // HALF
 LIST_COLS = HALF // 16
 WV_COLS = 256
@@ -41,51 +42,78 @@ def tile_list_gmu_tanh_none_kernel(
     with ExitStack() as ctx:
         keep = ctx.enter_context(tc.tile_pool(name="keep", bufs=1))
         work = ctx.enter_context(tc.tile_pool(name="work", bufs=8))
+        reuse = ctx.enter_context(tc.tile_pool(name="reuse", bufs=1))
         psum = ctx.enter_context(tc.psum_pool(name="psum", bufs=1))
 
         def held(shape, dtype, name):
             return keep.tile(shape, dtype, name=name, align_bytes=64)
 
+        def reused(shape, dtype, name, offset):
+            return reuse.tile(shape, dtype, name=name, align_bytes=64, offset=offset)
+
         list1 = held([P, J // 16], U16, "list1")
         list2 = held([P, J // 16], U16, "list2")
-        tab_s = held([P, T], U8, "tab_s")
+        raw_bytes = 4 * PACK * WV_COLS
+        raw_shape = [P, PACK, WV_COLS]
+        table_bytes = 4 * T
+        tab_w = reused([P, T], U32, "tab_w", 0)
+        tab_s = reused([P, T], U8, "tab_s", table_bytes - 64)
+        z_bytes = 2 * N + 4 * K_PASSES * N
+        raw00_at = table_bytes + T
+        z_at = raw00_at + J + 4 * HALF
+        z_w = reused([P, z_bytes], U8, "z_w", z_at)
+        zt_w = z_w[:, : 2 * N]
+        zv_w = z_w[:, 2 * N :].bitcast(U32).rearrange("p (a n) -> p a n", a=K_PASSES)
+        tab2_at = z_at + z_bytes
+        tab2_w = reused([P, T], U32, "tab2_w", tab2_at)
+        wv_raw = [
+            [reused(raw_shape, F32, "wv_raw00", raw00_at), held(raw_shape, F32, "wv_raw01")],
+            [reused(raw_shape, F32, "wv_raw1%d" % a, tab2_at + a * raw_bytes) for a in range(K_PASSES)],
+        ]
+        bf_at = tab2_at + table_bytes
+        wv_bf = [
+            held([P, K_PASSES, WV_COLS, PACK], BF16, "wv_bf0"),
+            reused([P, K_PASSES, WV_COLS, PACK], BF16, "wv_bf1", bf_at),
+        ]
+        pairs = held([P, HALF], U32, "pairs")
         tab2_s = held([P, T], U8, "tab2_s")
-        tab_w = held([P, T], U32, "tab_w")
-        tab2_w = held([P, T], U32, "tab2_w")
-        zv_w = held([P, K_PASSES, N], U32, "zv_w")
-        zv_s = held([P, K_PASSES, N], U8, "zv_s")
-        zt_w = held([P, 2 * N], U8, "zt_w")
-        zt_s = held([P, N], U8, "zt_s")
         wt_w = held([P, 2 * N], U8, "wt_w")
-        wt_s = held([P, N], U8, "wt_s")
+        weight_rows = held([BLOCKS, 4 * N], U8, "weight_rows")
+        weight_s = held([P, 4 * N], U8, "weight_s")
         bias = held([P, N // P], F32, "bias")
         half_bias = held([P, N // P], F32, "half_bias")
-        v_top = held([P, J], U8, "v_top")
-        v_s = held([P, K_PASSES, J], U8, "v_s")
-        v2_s = held([P, J], U8, "v2_s")
-        wv_raw = [[held([P, PACK, WV_COLS], F32, "wv_raw%d%d" % (g, a)) for a in range(K_PASSES)] for g in range(WV_PARTS)]
-        wv_bf = [held([P, K_PASSES, WV_COLS, PACK], BF16, "wv_bf%d" % g) for g in range(WV_PARTS)]
+        v_rows = held([P, J], U8, "v_rows")
+        v_s = [reused([P, J], U8, "v_s0", table_bytes), reused([P, J], U8, "v_s1", raw00_at)]
         wv_w = [held([P, K_PASSES * WV_COLS], U32, "wv_w%d" % g) for g in range(WV_PARTS)]
         wv_s = [held([P, K_PASSES * WV_COLS], U8, "wv_s%d" % g) for g in range(WV_PARTS)]
         v_w = [held([P, K_PASSES, 2 * HALF], U8, "v_w%d" % h) for h in range(HALVES)]
-        v2_w = [held([P, HALF], U32, "v2_w%d" % h) for h in range(HALVES)]
-        pairs = held([P, HALF], U32, "pairs")
-        banks = [psum.tile([P, HALF], F32, name="bank%d" % i) for i in range(2 * RING)]
+        v2_w = [held([P, HALF], U32, "v2_w0"), reused([P, HALF], U32, "v2_w1", raw00_at + J)]
+        after_rounding = {
+            ("diff", 0, 0): reused([P, HALF], F32, "first_diff", bf_at),
+        }
 
-        for q in range(QUADS):
-            nc.vector.memset(tab_s[QUAD * q : QUAD * q + TOP, :].bitcast(I32), 0)
-        two_passes = "p a n -> p (a n)"
-        for plane in (tab2_s[:], wt_s[:], v_s[:].rearrange(two_passes), zv_s[:].rearrange(two_passes), zt_s[:]):
-            nc.gpsimd.memset(plane.bitcast(I32), 0)
+        def result(kind, c, h):
+            if (kind, c, h) in after_rounding:
+                return after_rounding[kind, c, h]
+            return work.tile([P, HALF], F32, name=kind)
+
+        v2_s = [held([P, HALF], U8, "v2_s%d" % h) for h in range(HALVES)]
+        banks = [psum.tile([P, HALF], F32, name="bank%d" % i) for i in range(2 * RING)]
+        zv_s = [weight_s[:, a * N : (a + 1) * N] for a in range(K_PASSES)]
+        zt_s = weight_s[:, 2 * N : 3 * N]
+        wt_s = weight_s[:, 3 * N :]
+
+        nc.vector.memset(tab_s[0:LAST_QUAD, :].bitcast(I32), 0)
+        nc.gpsimd.memset(tab2_s[:].bitcast(I32), 0)
 
         def gather(dst, window, offsets):
             nc.vector.tensor_copy(dst, window[:].indirect(offsets))
 
-        def load_plane(tile, scales):
+        def load_plane(queue, tile, rows):
             for q in range(QUADS):
-                nc.sync.dma_start(
+                queue.dma_start(
                     out=tile[QUAD * q : QUAD * q + ROWS, :].bitcast(I32),
-                    in_=scales[0, ROWS * q : ROWS * (q + 1), :].bitcast(I32),
+                    in_=rows[ROWS * q : ROWS * (q + 1), :].bitcast(I32),
                 )
 
         def load_wv(g, a):
@@ -95,93 +123,101 @@ def tile_list_gmu_tanh_none_kernel(
         def load_table(tile, words):
             nc.sync.dma_start(out=tile[:].bitcast(I32), in_=words[0].rearrange("p t i -> p (t i)").bitcast(I32))
 
-        nc.sync.dma_start(list1[:], offs)
-        for q in range(QUADS):
-            nc.sync.dma_start(
-                out=tab_s[QUAD * q + TOP : QUAD * (q + 1), :].bitcast(I32),
-                in_=tab_scales[:, ROWS * q : ROWS * (q + 1), :].bitcast(I32),
-            )
-        load_wv(0, 0)
-        with nc.allow_non_contiguous_dma(reason="one bias value a partition"):
-            nc.sync.dma_start(out=bias[:], in_=b.rearrange("(c p) -> p c", p=P))
-        nc.sync.dma_start(list2[:], offs2)
-        load_plane(tab2_s, tab2_scales)
-        load_table(tab2_w, tab2_words)
-        load_wv(0, 1)
-        nc.sync.dma_start(out=wt_w[:].bitcast(I32), in_=wt_words[0].bitcast(I32))
-        load_plane(wt_s, wt_scales)
-        load_table(tab_w, tab_words)
-        gather(v_top[:], tab_s, list1[:])
-        for a in range(K_PASSES):
-            first = TOP + a * ROWS
-            nc.sync.dma_start(out=v_s[0:SPAN, a, :].bitcast(I32), in_=v_top[first : first + SPAN, :].bitcast(I32))
-        for q in range(QUADS):
-            nc.sync.dma_start(
-                out=zv_s[QUAD * q : QUAD * q + ROWS, :, :].bitcast(I32),
-                in_=zv_scales[:, ROWS * q : ROWS * (q + 1), :].rearrange("a r n -> r a n").bitcast(I32),
-            )
-        nc.sync.dma_start(out=zv_w[:].bitcast(I32), in_=zv_words.rearrange("a p n i -> p a (n i)").bitcast(I32))
-        nc.sync.dma_start(out=zt_w[:].bitcast(I32), in_=zt_words[0].bitcast(I32))
-        load_plane(zt_s, zt_scales)
-        load_wv(1, 0)
-        load_wv(1, 1)
-        nc.gpsimd.tensor_scalar(half_bias[:], bias[:], 0.5, 0.0, MULT, ADD)
-
         def half_list(lst, h):
             return lst[:, h * LIST_COLS : (h + 1) * LIST_COLS]
 
-        def round_wv(g):
-            for a in range(K_PASSES):
-                nc.scalar.copy(
-                    out=wv_bf[g][:, a].rearrange("p (c i) t -> p c t i", i=PACK),
-                    in_=wv_raw[g][a][:].rearrange("p t (c i) -> p c t i", i=PACK),
-                )
+        def round_wv(g, a):
+            nc.scalar.copy(
+                out=wv_bf[g][:, a].rearrange("p (c i) t -> p c t i", i=PACK),
+                in_=wv_raw[g][a][:].rearrange("p t (c i) -> p c t i", i=PACK),
+            )
 
         def quantise_wv(g):
             nc.vector.quantize_mx(
                 out=wv_w[g][:].bitcast(FP8X4), scales=wv_s[g][:], in_=wv_bf[g][:].rearrange("p a n t -> p (a n t)")
             )
 
-        def part(h):
+        def gather_text(h):
+            gather(v2_w[h][:], tab2_w, half_list(list2, h))
+            gather(v2_s[h][:], tab2_s, half_list(list2, h))
+
+        def gather_picture(h):
+            gather(pairs[:], tab_w, half_list(list1, h))
             nc.vector.tensor_copy(
                 out=v_w[h][:].bitcast(U16), in_=pairs[:].bitcast(U16).rearrange("p (j d) -> p d j", d=K_PASSES)
             )
 
-        gather(v2_s[:], tab2_s, list2[:])
-        for h in range(HALVES):
-            gather(v2_w[h][:], tab2_w, half_list(list2, h))
-        round_wv(0)
+        with nc.allow_non_contiguous_dma(reason="one bias value a partition"):
+            nc.gpsimd.dma_start(out=bias[:], in_=b.rearrange("(c p) -> p c", p=P))
+        nc.gpsimd.tensor_scalar(half_bias[:], bias[:], 0.5, 0.0, MULT, ADD)
+
+        def deal_picture_rows(moves):
+            for a, q in moves:
+                first = LAST_QUAD + BLOCKS * a + ROWS * q
+                nc.sync.dma_start(
+                    out=v_s[a][QUAD * q : QUAD * q + ROWS, :].bitcast(I32), in_=v_rows[first : first + ROWS, :].bitcast(I32)
+                )
+
+        nc.sync.dma_start(list1[:], offs)
+        nc.sync.dma_start(
+            out=tab_s[LAST_QUAD:, :].bitcast(I32), in_=tab_scales.rearrange("a r t -> (a r) t").bitcast(I32)
+        )
+        nc.sync.dma_start(list2[:], offs2)
+        nc.sync.dma_start(out=weight_rows[:, 3 * N :].bitcast(I32), in_=wt_scales[0].bitcast(I32))
+        nc.sync.dma_start(out=weight_rows[:, 2 * N : 3 * N].bitcast(I32), in_=zt_scales[0].bitcast(I32))
+        nc.sync.dma_start(
+            out=weight_rows[:, : 2 * N].rearrange("r (a n) -> r a n", a=K_PASSES).bitcast(I32),
+            in_=zv_scales.rearrange("a r n -> r a n").bitcast(I32),
+        )
+        load_table(tab2_w, tab2_words)
+        nc.sync.dma_start(out=wt_w[:].bitcast(I32), in_=wt_words[0].bitcast(I32))
+        load_plane(nc.sync, tab2_s, tab2_scales[0])
+        load_wv(0, 0)
+        load_wv(0, 1)
+        load_plane(nc.sync, weight_s, weight_rows)
+        gather(v_rows[:], tab_s, list1[:])
+        load_table(tab_w, tab_words)
+        moves = [(a, q) for a in range(K_PASSES) for q in range(QUADS)]
+        deal_picture_rows(moves[:FIRST_MOVES])
+        round_wv(0, 0)
+        nc.sync.dma_start(out=zv_w.bitcast(I32), in_=zv_words.rearrange("a p n i -> p a (n i)").bitcast(I32))
+        deal_picture_rows(moves[FIRST_MOVES:])
+        nc.sync.dma_start(out=zt_w.bitcast(I32), in_=zt_words[0].bitcast(I32))
+        round_wv(0, 1)
+        gather_text(0)
+        gather_text(1)
+        load_wv(1, 0)
+        load_wv(1, 1)
         quantise_wv(0)
-        for h in range(HALVES):
-            gather(pairs[:], tab_w, half_list(list1, h))
-            part(h)
+        gather_picture(0)
+        gather_picture(1)
 
         def text(h):
-            return dict(rhs=v2_w[h][:].bitcast(FP8X4), rhs_scale=v2_s[:, h * HALF : (h + 1) * HALF])
+            return dict(rhs=v2_w[h][:].bitcast(FP8X4), rhs_scale=v2_s[h][:])
 
         def picture(h, a):
-            return dict(rhs=v_w[h][:, a, :].bitcast(FP4X4), rhs_scale=v_s[:, a, h * HALF : (h + 1) * HALF])
+            return dict(rhs=v_w[h][:, a, :].bitcast(FP4X4), rhs_scale=v_s[a][:, h * HALF : (h + 1) * HALF])
 
         def make_at(c, h, bank):
             nc.tensor.matmul_mx(
                 out=bank[:], lhsT=wt_w[:, 2 * c * P : 2 * (c + 1) * P].bitcast(FP4X4), lhsT_scale=wt_s[:, c * P : (c + 1) * P],
                 start=True, stop=True, **text(h),
             )
-            at = work.tile([P, HALF], F32, name="at")
+            at = result("at", c, h)
             nc.scalar.activation(at[:], bank[:], TANH)
             return at
 
         def make_tg(c, h, bank):
             cols = slice(c * P, (c + 1) * P)
-            nc.tensor.matmul_mx(
-                out=bank[:], lhsT=zt_w[:, 2 * c * P : 2 * (c + 1) * P].bitcast(FP4X4), lhsT_scale=zt_s[:, cols],
-                start=True, stop=False, **text(h),
-            )
             for a in range(K_PASSES):
                 nc.tensor.matmul_mx(
-                    out=bank[:], lhsT=zv_w[:, a, cols].bitcast(FP8X4), lhsT_scale=zv_s[:, a, cols],
-                    start=False, stop=(a == K_PASSES - 1), **picture(h, a),
+                    out=bank[:], lhsT=zv_w[:, a, cols].bitcast(FP8X4), lhsT_scale=zv_s[a][:, cols],
+                    start=(a == 0), stop=False, **picture(h, a),
                 )
+            nc.tensor.matmul_mx(
+                out=bank[:], lhsT=zt_w[:, 2 * c * P : 2 * (c + 1) * P].bitcast(FP4X4), lhsT_scale=zt_s[:, cols],
+                start=False, stop=True, **text(h),
+            )
             tg = work.tile([P, HALF], F32, name="tg")
             nc.scalar.activation(tg[:], bank[:], TANH, bias=half_bias[:, c : c + 1], scale=0.5)
             return tg
@@ -194,7 +230,7 @@ def tile_list_gmu_tanh_none_kernel(
                     out=bank[:], lhsT=wv_w[g][:, wcols].bitcast(FP8X4), lhsT_scale=wv_s[g][:, wcols],
                     start=(a == 0), stop=(a == K_PASSES - 1), **picture(h, a),
                 )
-            av = work.tile([P, HALF], F32, name="av")
+            av = result("av", c, h)
             nc.scalar.activation(av[:], bank[:], TANH)
             return av
 
@@ -210,31 +246,38 @@ def tile_list_gmu_tanh_none_kernel(
             made[kind, c, h] = maker(c, h, banks[RING * (max(pair - 1, 0) % 2) + turn])
             turns.append(kind)
 
-        def blend(g, h):
-            chunks = range(g * CHUNKS, (g + 1) * CHUNKS)
-            for c in chunks:
-                if ("at", c, h) not in made:
-                    made["at", c, h] = make_at(c, h, banks[RING])
-                if g == 0 and h == 0:
-                    in_ring("av", make_av, c, h)
-                    in_ring("tg", make_tg, c, h)
-                else:
-                    in_ring("tg", make_tg, c, h)
-                    in_ring("av", make_av, c, h)
-            diffs = [work.tile([P, HALF], F32, name="diff") for c in chunks]
-            gated = [work.tile([P, HALF], F32, name="gated") for c in chunks]
-            res = [work.tile([P, HALF], F32, name="res") for c in chunks]
-            for c, d in zip(chunks, diffs):
-                nc.vector.tensor_tensor(d[:], made["av", c, h][:], made["at", c, h][:], SUB)
-            for c, d, m in zip(chunks, diffs, gated):
-                nc.vector.scalar_tensor_tensor(m[:], made["tg", c, h][:], 1.0, d[:], ADD, MULT)
-            for c, m, r in zip(chunks, gated, res):
-                nc.vector.scalar_tensor_tensor(r[:], m[:], 0.5, made["at", c, h][:], MULT, ADD)
-                made["res", c, h] = r
-                nc.sync.dma_start(out=out[c * P : (c + 1) * P, h * HALF : (h + 1) * HALF], in_=r[:])
+        order = [(c, h) for g in range(WV_PARTS) for h in range(HALVES) for c in range(g * CHUNKS, (g + 1) * CHUNKS)]
 
-        round_wv(1)
-        quantise_wv(1)
-        for g in range(WV_PARTS):
-            for h in range(HALVES):
-                blend(g, h)
+        def products(c, h):
+            if ("at", c, h) not in made:
+                made["at", c, h] = make_at(c, h, banks[RING])
+            in_ring("av", make_av, c, h)
+            in_ring("tg", make_tg, c, h)
+
+        def differ(c, h):
+            made["diff", c, h] = result("diff", c, h)
+            nc.vector.tensor_tensor(made["diff", c, h][:], made["av", c, h][:], made["at", c, h][:], SUB)
+
+        def gate(c, h):
+            made["gated", c, h] = result("gated", c, h)
+            nc.vector.scalar_tensor_tensor(
+                made["gated", c, h][:], made["tg", c, h][:], 1.0, made["diff", c, h][:], ADD, MULT
+            )
+
+        def finish(c, h):
+            res = result("res", c, h)
+            nc.vector.scalar_tensor_tensor(res[:], made["gated", c, h][:], 0.5, made["at", c, h][:], MULT, ADD)
+            nc.sync.dma_start(out=out[c * P : (c + 1) * P, h * HALF : (h + 1) * HALF], in_=res[:])
+
+        products(*order[0])
+        differ(*order[0])
+        for i, tile in enumerate(order):
+            gate(*tile)
+            if i == 0:
+                for a in range(K_PASSES):
+                    round_wv(1, a)
+                quantise_wv(1)
+            if i + 1 < len(order):
+                products(*order[i + 1])
+                differ(*order[i + 1])
+            finish(*tile)

@@ -25,8 +25,8 @@ BLOCKS = QUADS * ROWS
 LAST_QUAD = QUAD * (QUADS - 1)
 HALF = 512
 RING = 4
-FIRST_MOVES = 4
-EARLY = 7
+FIRST_MOVES = 6
+EARLY = 8
 HALVES = J // HALF
 LIST_COLS = HALF // 16
 WV_COLS = 256
@@ -57,20 +57,20 @@ def tile_list_gmu_tanh_none_kernel(
         raw_shape = [P, PACK, WV_COLS]
         table_bytes = 4 * T
         tab_w = reused([P, T], U32, "tab_w", 0)
-        tab_s = reused([P, T], U8, "tab_s", table_bytes - 64)
+        tab_s = reused([P, T], U8, "tab_s", table_bytes - T // 2)
         z_bytes = 2 * N + 4 * K_PASSES * N
-        raw00_at = table_bytes + T
-        z_at = raw00_at + J + 4 * HALF
+        z_at = table_bytes
+        raw00_at = z_at + z_bytes
         z_w = reused([P, z_bytes], U8, "z_w", z_at)
         zt_w = z_w[:, : 2 * N]
         zv_w = z_w[:, 2 * N :].bitcast(U32).rearrange("p (a n) -> p a n", a=K_PASSES)
-        tab2_at = z_at + z_bytes
+        tab2_at = raw00_at + raw_bytes
         tab2_w = reused([P, T], U32, "tab2_w", tab2_at)
         wv_raw = [
             [reused(raw_shape, F32, "wv_raw00", raw00_at), held(raw_shape, F32, "wv_raw01")],
-            [reused(raw_shape, F32, "wv_raw1%d" % a, tab2_at + a * raw_bytes) for a in range(K_PASSES)],
+            [reused(raw_shape, F32, "wv_raw1%d" % a, tab2_at + 64 + a * raw_bytes) for a in range(K_PASSES)],
         ]
-        bf_at = tab2_at + table_bytes
+        bf_at = tab2_at + table_bytes + 64
         wv_bf = [
             held([P, K_PASSES, WV_COLS, PACK], BF16, "wv_bf0"),
             reused([P, K_PASSES, WV_COLS, PACK], BF16, "wv_bf1", bf_at),
@@ -80,14 +80,14 @@ def tile_list_gmu_tanh_none_kernel(
         wt_w = held([P, 2 * N], U8, "wt_w")
         weight_rows = held([BLOCKS, 4 * N], U8, "weight_rows")
         weight_s = held([P, 4 * N], U8, "weight_s")
-        bias = held([P, N // P], F32, "bias")
+        bias = reused([P, N // P], F32, "bias", tab2_at)
         half_bias = held([P, N // P], F32, "half_bias")
         v_rows = held([P, J], U8, "v_rows")
-        v_s = [reused([P, J], U8, "v_s0", table_bytes), reused([P, J], U8, "v_s1", raw00_at)]
+        v_s = [held([P, J], U8, "v_s%d" % a) for a in range(K_PASSES)]
         wv_w = [held([P, K_PASSES * WV_COLS], U32, "wv_w%d" % g) for g in range(WV_PARTS)]
         wv_s = [held([P, K_PASSES * WV_COLS], U8, "wv_s%d" % g) for g in range(WV_PARTS)]
         v_w = [held([P, K_PASSES, 2 * HALF], U8, "v_w%d" % h) for h in range(HALVES)]
-        v2_w = [held([P, HALF], U32, "v2_w0"), reused([P, HALF], U32, "v2_w1", raw00_at + J)]
+        v2_w = [held([P, HALF], U32, "v2_w0"), reused([P, HALF], U32, "v2_w1", raw00_at)]
         after_rounding = {
             ("diff", 0, 0): reused([P, HALF], F32, "first_diff", bf_at),
         }
@@ -147,9 +147,6 @@ def tile_list_gmu_tanh_none_kernel(
                 out=v_w[h][:].bitcast(U16), in_=pairs[:].bitcast(U16).rearrange("p (j d) -> p d j", d=K_PASSES)
             )
 
-        with nc.allow_non_contiguous_dma(reason="one bias value a partition"):
-            nc.gpsimd.dma_start(out=bias[:], in_=b.rearrange("(c p) -> p c", p=P))
-        nc.gpsimd.tensor_scalar(half_bias[:], bias[:], 0.5, 0.0, MULT, ADD)
 
         def deal_picture_rows(moves):
             for a, q in moves:
@@ -186,6 +183,9 @@ def tile_list_gmu_tanh_none_kernel(
         round_wv(0, 1)
         gather_text(0)
         gather_text(1)
+        with nc.allow_non_contiguous_dma(reason="one bias value a partition"):
+            nc.sync.dma_start(out=bias[:], in_=b.rearrange("(c p) -> p c", p=P))
+        nc.scalar.mul(half_bias[:], bias[:], 0.5)
         load_wv(1, 0)
         load_wv(1, 1)
         quantise_wv(0)
@@ -209,26 +209,26 @@ def tile_list_gmu_tanh_none_kernel(
 
         def make_tg(c, h, bank):
             cols = slice(c * P, (c + 1) * P)
-            for a in range(K_PASSES):
-                nc.tensor.matmul_mx(
-                    out=bank[:], lhsT=zv_w[:, a, cols].bitcast(FP8X4), lhsT_scale=zv_s[a][:, cols],
-                    start=(a == 0), stop=False, **picture(h, a),
-                )
             nc.tensor.matmul_mx(
                 out=bank[:], lhsT=zt_w[:, 2 * c * P : 2 * (c + 1) * P].bitcast(FP4X4), lhsT_scale=zt_s[:, cols],
-                start=False, stop=True, **text(h),
+                start=True, stop=False, **text(h),
             )
+            for a in reversed(range(K_PASSES)):
+                nc.tensor.matmul_mx(
+                    out=bank[:], lhsT=zv_w[:, a, cols].bitcast(FP8X4), lhsT_scale=zv_s[a][:, cols],
+                    start=False, stop=(a == 0), **picture(h, a),
+                )
             tg = work.tile([P, HALF], F32, name="tg")
             nc.scalar.activation(tg[:], bank[:], TANH, bias=half_bias[:, c : c + 1], scale=0.5)
             return tg
 
         def make_av(c, h, bank):
             g, cc = divmod(c, CHUNKS)
-            for a in range(K_PASSES):
+            for a in reversed(range(K_PASSES)):
                 wcols = slice(a * WV_COLS + cc * P, a * WV_COLS + (cc + 1) * P)
                 nc.tensor.matmul_mx(
                     out=bank[:], lhsT=wv_w[g][:, wcols].bitcast(FP8X4), lhsT_scale=wv_s[g][:, wcols],
-                    start=(a == 0), stop=(a == K_PASSES - 1), **picture(h, a),
+                    start=(a == K_PASSES - 1), stop=(a == 0), **picture(h, a),
                 )
             av = result("av", c, h)
             nc.scalar.activation(av[:], bank[:], TANH)
@@ -246,38 +246,33 @@ def tile_list_gmu_tanh_none_kernel(
             made[kind, c, h] = maker(c, h, banks[RING * (max(pair - 1, 0) % 2) + turn])
             turns.append(kind)
 
-        order = [(c, h) for g in range(WV_PARTS) for h in range(HALVES) for c in range(g * CHUNKS, (g + 1) * CHUNKS)]
+        def blend(g, h):
+            chunks = range(g * CHUNKS, (g + 1) * CHUNKS)
+            for c in chunks:
+                if ("at", c, h) not in made:
+                    made["at", c, h] = make_at(c, h, banks[RING])
+                if g == 0 and h == 0:
+                    in_ring("av", make_av, c, h)
+                    in_ring("tg", make_tg, c, h)
+                else:
+                    in_ring("tg", make_tg, c, h)
+                    in_ring("av", make_av, c, h)
+            diffs = [result("diff", c, h) for c in chunks]
+            gated = [work.tile([P, HALF], F32, name="gated") for c in chunks]
+            res = [work.tile([P, HALF], F32, name="res") for c in chunks]
+            for c, d in zip(chunks, diffs):
+                nc.vector.tensor_tensor(d[:], made["av", c, h][:], made["at", c, h][:], SUB)
+            for c, d, m in zip(chunks, diffs, gated):
+                nc.vector.scalar_tensor_tensor(m[:], made["tg", c, h][:], 1.0, d[:], ADD, MULT)
+            for c, m, r in zip(chunks, gated, res):
+                nc.vector.scalar_tensor_tensor(r[:], m[:], 0.5, made["at", c, h][:], MULT, ADD)
+                made["res", c, h] = r
+                nc.sync.dma_start(out=out[c * P : (c + 1) * P, h * HALF : (h + 1) * HALF], in_=r[:])
 
-        def products(c, h):
-            if ("at", c, h) not in made:
-                made["at", c, h] = make_at(c, h, banks[RING])
-            in_ring("av", make_av, c, h)
-            in_ring("tg", make_tg, c, h)
-
-        def differ(c, h):
-            made["diff", c, h] = result("diff", c, h)
-            nc.vector.tensor_tensor(made["diff", c, h][:], made["av", c, h][:], made["at", c, h][:], SUB)
-
-        def gate(c, h):
-            made["gated", c, h] = result("gated", c, h)
-            nc.vector.scalar_tensor_tensor(
-                made["gated", c, h][:], made["tg", c, h][:], 1.0, made["diff", c, h][:], ADD, MULT
-            )
-
-        def finish(c, h):
-            res = result("res", c, h)
-            nc.vector.scalar_tensor_tensor(res[:], made["gated", c, h][:], 0.5, made["at", c, h][:], MULT, ADD)
-            nc.sync.dma_start(out=out[c * P : (c + 1) * P, h * HALF : (h + 1) * HALF], in_=res[:])
-
-        products(*order[0])
-        differ(*order[0])
-        for i, tile in enumerate(order):
-            gate(*tile)
-            if i == 0:
-                for a in range(K_PASSES):
-                    round_wv(1, a)
-                quantise_wv(1)
-            if i + 1 < len(order):
-                products(*order[i + 1])
-                differ(*order[i + 1])
-            finish(*tile)
+        for g in range(WV_PARTS):
+            for h in range(HALVES):
+                blend(g, h)
+                if g == 0 and h == 0:
+                    for a in range(K_PASSES):
+                        round_wv(1, a)
+                    quantise_wv(1)

@@ -25,8 +25,8 @@ BLOCKS = QUADS * ROWS
 LAST_QUAD = QUAD * (QUADS - 1)
 HALF = 512
 RING = 4
-FIRST_MOVES = 6
-EARLY = 8
+FIRST_MOVES = 2
+EARLY = 7
 HALVES = J // HALF
 LIST_COLS = HALF // 16
 WV_COLS = 256
@@ -56,10 +56,11 @@ def tile_list_gmu_tanh_none_kernel(
         raw_bytes = 4 * PACK * WV_COLS
         raw_shape = [P, PACK, WV_COLS]
         table_bytes = 4 * T
-        tab_w = reused([P, T], U32, "tab_w", 0)
-        tab_s = reused([P, T], U8, "tab_s", table_bytes - T // 2)
+        tab_w = held([P, T], U32, "tab_w")
+        tab_s = reused([P, T], U8, "tab_s", 0)
+        z_s = reused([P, 3 * N], U8, "z_s", 0)
         z_bytes = 2 * N + 4 * K_PASSES * N
-        z_at = table_bytes
+        z_at = 3 * N
         raw00_at = z_at + z_bytes
         z_w = reused([P, z_bytes], U8, "z_w", z_at)
         zt_w = z_w[:, : 2 * N]
@@ -73,13 +74,13 @@ def tile_list_gmu_tanh_none_kernel(
         bf_at = tab2_at + table_bytes + 64
         wv_bf = [
             held([P, K_PASSES, WV_COLS, PACK], BF16, "wv_bf0"),
-            reused([P, K_PASSES, WV_COLS, PACK], BF16, "wv_bf1", bf_at),
+            held([P, K_PASSES, WV_COLS, PACK], BF16, "wv_bf1"),
         ]
         pairs = held([P, HALF], U32, "pairs")
         tab2_s = held([P, T], U8, "tab2_s")
         wt_w = held([P, 2 * N], U8, "wt_w")
-        weight_rows = held([BLOCKS, 4 * N], U8, "weight_rows")
-        weight_s = held([P, 4 * N], U8, "weight_s")
+        wt_s = held([P, N], U8, "wt_s")
+        z_rows = held([BLOCKS, 3 * N], U8, "z_rows")
         bias = reused([P, N // P], F32, "bias", tab2_at)
         half_bias = held([P, N // P], F32, "half_bias")
         v_rows = held([P, J], U8, "v_rows")
@@ -87,9 +88,8 @@ def tile_list_gmu_tanh_none_kernel(
         wv_w = [held([P, K_PASSES * WV_COLS], U32, "wv_w%d" % g) for g in range(WV_PARTS)]
         wv_s = [held([P, K_PASSES * WV_COLS], U8, "wv_s%d" % g) for g in range(WV_PARTS)]
         v_w = [held([P, K_PASSES, 2 * HALF], U8, "v_w%d" % h) for h in range(HALVES)]
-        v2_w = [held([P, HALF], U32, "v2_w0"), reused([P, HALF], U32, "v2_w1", raw00_at)]
+        v2_w = [held([P, HALF], U32, "v2_w0"), held([P, HALF], U32, "v2_w1")]
         after_rounding = {
-            ("diff", 0, 0): reused([P, HALF], F32, "first_diff", bf_at),
         }
 
         def result(kind, c, h):
@@ -97,11 +97,11 @@ def tile_list_gmu_tanh_none_kernel(
                 return after_rounding[kind, c, h]
             return work.tile([P, HALF], F32, name=kind)
 
-        v2_s = [held([P, HALF], U8, "v2_s%d" % h) for h in range(HALVES)]
+        v2_all = held([P, J], U8, "v2_all")
+        v2_s = [v2_all[:, h * HALF : (h + 1) * HALF] for h in range(HALVES)]
         banks = [psum.tile([P, HALF], F32, name="bank%d" % i) for i in range(2 * RING)]
-        zv_s = [weight_s[:, a * N : (a + 1) * N] for a in range(K_PASSES)]
-        zt_s = weight_s[:, 2 * N : 3 * N]
-        wt_s = weight_s[:, 3 * N :]
+        zv_s = [z_s[:, a * N : (a + 1) * N] for a in range(K_PASSES)]
+        zt_s = z_s[:, 2 * N :]
 
         nc.vector.memset(tab_s[0:LAST_QUAD, :].bitcast(I32), 0)
         nc.gpsimd.memset(tab2_s[:].bitcast(I32), 0)
@@ -109,8 +109,8 @@ def tile_list_gmu_tanh_none_kernel(
         def gather(dst, window, offsets):
             nc.vector.tensor_copy(dst, window[:].indirect(offsets))
 
-        def load_plane(queue, tile, rows):
-            for q in range(QUADS):
+        def load_plane(queue, tile, rows, quads=range(QUADS)):
+            for q in quads:
                 queue.dma_start(
                     out=tile[QUAD * q : QUAD * q + ROWS, :].bitcast(I32),
                     in_=rows[ROWS * q : ROWS * (q + 1), :].bitcast(I32),
@@ -139,7 +139,6 @@ def tile_list_gmu_tanh_none_kernel(
 
         def gather_text(h):
             gather(v2_w[h][:], tab2_w, half_list(list2, h))
-            gather(v2_s[h][:], tab2_s, half_list(list2, h))
 
         def gather_picture(h):
             gather(pairs[:], tab_w, half_list(list1, h))
@@ -160,27 +159,30 @@ def tile_list_gmu_tanh_none_kernel(
             out=tab_s[LAST_QUAD:, :].bitcast(I32), in_=tab_scales.rearrange("a r t -> (a r) t").bitcast(I32)
         )
         nc.sync.dma_start(list2[:], offs2)
-        nc.sync.dma_start(out=weight_rows[:, 3 * N :].bitcast(I32), in_=wt_scales[0].bitcast(I32))
-        nc.sync.dma_start(out=weight_rows[:, 2 * N : 3 * N].bitcast(I32), in_=zt_scales[0].bitcast(I32))
+        load_plane(nc.sync, wt_s, wt_scales[0], range(2))
+        load_wv(0, 0)
+        nc.sync.dma_start(out=wt_w[:].bitcast(I32), in_=wt_words[0].bitcast(I32))
+        load_plane(nc.sync, wt_s, wt_scales[0], range(2, 3))
+        load_plane(nc.sync, tab2_s, tab2_scales[0])
+        load_table(tab2_w, tab2_words)
+        load_wv(0, 1)
+        load_plane(nc.sync, wt_s, wt_scales[0], range(3, 4))
+        load_table(tab_w, tab_words)
+        nc.sync.dma_start(out=z_rows[:, 2 * N :].bitcast(I32), in_=zt_scales[0].bitcast(I32))
         nc.sync.dma_start(
-            out=weight_rows[:, : 2 * N].rearrange("r (a n) -> r a n", a=K_PASSES).bitcast(I32),
+            out=z_rows[:, : 2 * N].rearrange("r (a n) -> r a n", a=K_PASSES).bitcast(I32),
             in_=zv_scales.rearrange("a r n -> r a n").bitcast(I32),
         )
-        load_table(tab2_w, tab2_words)
-        nc.sync.dma_start(out=wt_w[:].bitcast(I32), in_=wt_words[0].bitcast(I32))
-        load_plane(nc.sync, tab2_s, tab2_scales[0])
-        load_wv(0, 0)
-        load_wv(0, 1)
-        load_plane(nc.sync, weight_s, weight_rows)
         gather(v_rows[:], tab_s, list1[:])
-        load_table(tab_w, tab_words)
         moves = [(a, q) for a in range(K_PASSES) for q in range(QUADS)]
         deal_picture_rows(moves[:FIRST_MOVES])
         round_wv(0, 0)
         nc.sync.dma_start(out=zv_w.bitcast(I32), in_=zv_words.rearrange("a p n i -> p a (n i)").bitcast(I32))
-        deal_picture_rows(moves[FIRST_MOVES:])
         nc.sync.dma_start(out=zt_w.bitcast(I32), in_=zt_words[0].bitcast(I32))
+        deal_picture_rows(moves[FIRST_MOVES:])
+        load_plane(nc.sync, z_s, z_rows)
         round_wv(0, 1)
+        gather(v2_all[:], tab2_s, list2[:])
         gather_text(0)
         gather_text(1)
         with nc.allow_non_contiguous_dma(reason="one bias value a partition"):
@@ -193,7 +195,7 @@ def tile_list_gmu_tanh_none_kernel(
         gather_picture(1)
 
         def text(h):
-            return dict(rhs=v2_w[h][:].bitcast(FP8X4), rhs_scale=v2_s[h][:])
+            return dict(rhs=v2_w[h][:].bitcast(FP8X4), rhs_scale=v2_s[h])
 
         def picture(h, a):
             return dict(rhs=v_w[h][:, a, :].bitcast(FP4X4), rhs_scale=v_s[a][:, h * HALF : (h + 1) * HALF])
@@ -269,10 +271,9 @@ def tile_list_gmu_tanh_none_kernel(
                 made["res", c, h] = r
                 nc.sync.dma_start(out=out[c * P : (c + 1) * P, h * HALF : (h + 1) * HALF], in_=r[:])
 
+        for a in range(K_PASSES):
+            round_wv(1, a)
+        quantise_wv(1)
         for g in range(WV_PARTS):
             for h in range(HALVES):
                 blend(g, h)
-                if g == 0 and h == 0:
-                    for a in range(K_PASSES):
-                        round_wv(1, a)
-                    quantise_wv(1)

@@ -25,8 +25,8 @@ BLOCKS = QUADS * ROWS
 LAST_QUAD = QUAD * (QUADS - 1)
 HALF = 512
 RING = 4
-FIRST_MOVES = 2
-EARLY = 7
+FIRST_MOVES = 1
+EARLY = 8
 HALVES = J // HALF
 LIST_COLS = HALF // 16
 WV_COLS = 256
@@ -53,35 +53,24 @@ def tile_list_gmu_tanh_none_kernel(
 
         list1 = held([P, J // 16], U16, "list1")
         list2 = held([P, J // 16], U16, "list2")
-        raw_bytes = 4 * PACK * WV_COLS
         raw_shape = [P, PACK, WV_COLS]
-        table_bytes = 4 * T
         tab_w = held([P, T], U32, "tab_w")
-        tab_s = reused([P, T], U8, "tab_s", 0)
-        z_s = reused([P, 3 * N], U8, "z_s", 0)
-        z_bytes = 2 * N + 4 * K_PASSES * N
-        z_at = 3 * N
-        raw00_at = z_at + z_bytes
-        z_w = reused([P, z_bytes], U8, "z_w", z_at)
-        zt_w = z_w[:, : 2 * N]
-        zv_w = z_w[:, 2 * N :].bitcast(U32).rearrange("p (a n) -> p a n", a=K_PASSES)
-        tab2_at = raw00_at + raw_bytes
-        tab2_w = reused([P, T], U32, "tab2_w", tab2_at)
-        wv_raw = [
-            [reused(raw_shape, F32, "wv_raw00", raw00_at), held(raw_shape, F32, "wv_raw01")],
-            [reused(raw_shape, F32, "wv_raw1%d" % a, tab2_at + 64 + a * raw_bytes) for a in range(K_PASSES)],
-        ]
-        bf_at = tab2_at + table_bytes + 64
-        wv_bf = [
-            held([P, K_PASSES, WV_COLS, PACK], BF16, "wv_bf0"),
-            held([P, K_PASSES, WV_COLS, PACK], BF16, "wv_bf1"),
-        ]
-        pairs = held([P, HALF], U32, "pairs")
+        tab_s = held([P, T], U8, "tab_s")
+        z_s = held([P, 4 * N], U8, "z_s")
+        zt_w = held([P, 2 * N], U8, "zt_w")
+        zv_w = held([P, K_PASSES, N], U32, "zv_w")
+        tab2_w = held([P, T], U32, "tab2_w")
+        wv_raw = [[held(raw_shape, F32, "wv_raw%d%d" % (g, a)) for a in range(K_PASSES)] for g in range(WV_PARTS)]
+        tile_bytes = 4 * HALF
+        wv_bf0 = held([P, K_PASSES, WV_COLS, PACK], BF16, "wv_bf0")
+        wv_bf1 = reused([P, K_PASSES, WV_COLS, PACK], BF16, "wv_bf1", 0)
+        wv_bf = [[t[:, a] for a in range(K_PASSES)] for t in (wv_bf0, wv_bf1)]
+        pairs = [held([P, HALF // 2], U32, "pairs%d" % i) for i in range(2)]
         tab2_s = held([P, T], U8, "tab2_s")
         wt_w = held([P, 2 * N], U8, "wt_w")
-        wt_s = held([P, N], U8, "wt_s")
-        z_rows = held([BLOCKS, 3 * N], U8, "z_rows")
-        bias = reused([P, N // P], F32, "bias", tab2_at)
+        wt_s = z_s[:, 3 * N :]
+        z_rows = held([BLOCKS, 4 * N], U8, "z_rows")
+        bias = held([P, N // P], F32, "bias")
         half_bias = held([P, N // P], F32, "half_bias")
         v_rows = held([P, J], U8, "v_rows")
         v_s = [held([P, J], U8, "v_s%d" % a) for a in range(K_PASSES)]
@@ -90,6 +79,8 @@ def tile_list_gmu_tanh_none_kernel(
         v_w = [held([P, K_PASSES, 2 * HALF], U8, "v_w%d" % h) for h in range(HALVES)]
         v2_w = [held([P, HALF], U32, "v2_w0"), held([P, HALF], U32, "v2_w1")]
         after_rounding = {
+            ("diff", 0, 0): reused([P, HALF], F32, "diff00", 0),
+            ("tg", 0, 0): reused([P, HALF], F32, "tg00", tile_bytes),
         }
 
         def result(kind, c, h):
@@ -101,7 +92,7 @@ def tile_list_gmu_tanh_none_kernel(
         v2_s = [v2_all[:, h * HALF : (h + 1) * HALF] for h in range(HALVES)]
         banks = [psum.tile([P, HALF], F32, name="bank%d" % i) for i in range(2 * RING)]
         zv_s = [z_s[:, a * N : (a + 1) * N] for a in range(K_PASSES)]
-        zt_s = z_s[:, 2 * N :]
+        zt_s = z_s[:, 2 * N : 3 * N]
 
         nc.vector.memset(tab_s[0:LAST_QUAD, :].bitcast(I32), 0)
         nc.gpsimd.memset(tab2_s[:].bitcast(I32), 0)
@@ -128,23 +119,32 @@ def tile_list_gmu_tanh_none_kernel(
 
         def round_wv(g, a):
             nc.scalar.copy(
-                out=wv_bf[g][:, a].rearrange("p (c i) t -> p c t i", i=PACK),
+                out=wv_bf[g][a].rearrange("p (c i) t -> p c t i", i=PACK),
                 in_=wv_raw[g][a][:].rearrange("p t (c i) -> p c t i", i=PACK),
             )
 
-        def quantise_wv(g):
+        def quantise_first():
             nc.vector.quantize_mx(
-                out=wv_w[g][:].bitcast(FP8X4), scales=wv_s[g][:], in_=wv_bf[g][:].rearrange("p a n t -> p (a n t)")
+                out=wv_w[0][:].bitcast(FP8X4), scales=wv_s[0][:], in_=wv_bf0[:].rearrange("p a n t -> p (a n t)")
+            )
+
+        def quantise_late():
+            nc.vector.quantize_mx(
+                out=wv_w[1][:].bitcast(FP8X4), scales=wv_s[1][:], in_=wv_bf1[:].rearrange("p a n t -> p (a n t)")
             )
 
         def gather_text(h):
             gather(v2_w[h][:], tab2_w, half_list(list2, h))
 
         def gather_picture(h):
-            gather(pairs[:], tab_w, half_list(list1, h))
-            nc.vector.tensor_copy(
-                out=v_w[h][:].bitcast(U16), in_=pairs[:].bitcast(U16).rearrange("p (j d) -> p d j", d=K_PASSES)
-            )
+            for i in range(2):
+                first = h * LIST_COLS + i * LIST_COLS // 2
+                gather(pairs[i][:], tab_w, list1[:, first : first + LIST_COLS // 2])
+            for i in range(2):
+                nc.vector.tensor_copy(
+                    out=v_w[h][:].bitcast(U16)[:, :, i * HALF // 2 : (i + 1) * HALF // 2],
+                    in_=pairs[i][:].bitcast(U16).rearrange("p (j d) -> p d j", d=K_PASSES),
+                )
 
 
         def deal_picture_rows(moves):
@@ -159,38 +159,37 @@ def tile_list_gmu_tanh_none_kernel(
             out=tab_s[LAST_QUAD:, :].bitcast(I32), in_=tab_scales.rearrange("a r t -> (a r) t").bitcast(I32)
         )
         nc.sync.dma_start(list2[:], offs2)
-        load_plane(nc.sync, wt_s, wt_scales[0], range(2))
-        load_wv(0, 0)
-        nc.sync.dma_start(out=wt_w[:].bitcast(I32), in_=wt_words[0].bitcast(I32))
-        load_plane(nc.sync, wt_s, wt_scales[0], range(2, 3))
-        load_plane(nc.sync, tab2_s, tab2_scales[0])
-        load_table(tab2_w, tab2_words)
-        load_wv(0, 1)
-        load_plane(nc.sync, wt_s, wt_scales[0], range(3, 4))
-        load_table(tab_w, tab_words)
-        nc.sync.dma_start(out=z_rows[:, 2 * N :].bitcast(I32), in_=zt_scales[0].bitcast(I32))
         nc.sync.dma_start(
             out=z_rows[:, : 2 * N].rearrange("r (a n) -> r a n", a=K_PASSES).bitcast(I32),
             in_=zv_scales.rearrange("a r n -> r a n").bitcast(I32),
         )
+        nc.sync.dma_start(out=z_rows[:, 2 * N : 3 * N].bitcast(I32), in_=zt_scales[0].bitcast(I32))
+        nc.sync.dma_start(out=z_rows[:, 3 * N :].bitcast(I32), in_=wt_scales[0].bitcast(I32))
+        load_wv(0, 0)
+        nc.sync.dma_start(out=wt_w[:].bitcast(I32), in_=wt_words[0].bitcast(I32))
+        load_plane(nc.sync, tab2_s, tab2_scales[0])
+        load_table(tab2_w, tab2_words)
+        load_wv(0, 1)
+        load_plane(nc.sync, z_s, z_rows)
         gather(v_rows[:], tab_s, list1[:])
         moves = [(a, q) for a in range(K_PASSES) for q in range(QUADS)]
         deal_picture_rows(moves[:FIRST_MOVES])
+        load_table(tab_w, tab_words)
+        deal_picture_rows(moves[FIRST_MOVES:-1])
+        nc.sync.dma_start(out=zv_w[:].bitcast(I32), in_=zv_words.rearrange("a p n i -> p a (n i)").bitcast(I32))
+        deal_picture_rows(moves[-1:])
+        nc.sync.dma_start(out=zt_w[:].bitcast(I32), in_=zt_words[0].bitcast(I32))
+        with nc.allow_non_contiguous_dma(reason="one bias value a partition"):
+            nc.sync.dma_start(out=bias[:], in_=b.rearrange("(c p) -> p c", p=P))
+        load_wv(1, 0)
+        load_wv(1, 1)
         round_wv(0, 0)
-        nc.sync.dma_start(out=zv_w.bitcast(I32), in_=zv_words.rearrange("a p n i -> p a (n i)").bitcast(I32))
-        nc.sync.dma_start(out=zt_w.bitcast(I32), in_=zt_words[0].bitcast(I32))
-        deal_picture_rows(moves[FIRST_MOVES:])
-        load_plane(nc.sync, z_s, z_rows)
         round_wv(0, 1)
         gather(v2_all[:], tab2_s, list2[:])
         gather_text(0)
         gather_text(1)
-        with nc.allow_non_contiguous_dma(reason="one bias value a partition"):
-            nc.sync.dma_start(out=bias[:], in_=b.rearrange("(c p) -> p c", p=P))
+        quantise_first()
         nc.scalar.mul(half_bias[:], bias[:], 0.5)
-        load_wv(1, 0)
-        load_wv(1, 1)
-        quantise_wv(0)
         gather_picture(0)
         gather_picture(1)
 
@@ -220,7 +219,7 @@ def tile_list_gmu_tanh_none_kernel(
                     out=bank[:], lhsT=zv_w[:, a, cols].bitcast(FP8X4), lhsT_scale=zv_s[a][:, cols],
                     start=False, stop=(a == 0), **picture(h, a),
                 )
-            tg = work.tile([P, HALF], F32, name="tg")
+            tg = result("tg", c, h)
             nc.scalar.activation(tg[:], bank[:], TANH, bias=half_bias[:, c : c + 1], scale=0.5)
             return tg
 
@@ -248,32 +247,38 @@ def tile_list_gmu_tanh_none_kernel(
             made[kind, c, h] = maker(c, h, banks[RING * (max(pair - 1, 0) % 2) + turn])
             turns.append(kind)
 
+        def products(kind, maker, g, h):
+            for c in range(g * CHUNKS, (g + 1) * CHUNKS):
+                in_ring(kind, maker, c, h)
+
+        def differences(g, h):
+            for c in range(g * CHUNKS, (g + 1) * CHUNKS):
+                made["diff", c, h] = result("diff", c, h)
+                nc.vector.tensor_tensor(made["diff", c, h][:], made["av", c, h][:], made["at", c, h][:], SUB)
+
         def blend(g, h):
             chunks = range(g * CHUNKS, (g + 1) * CHUNKS)
-            for c in chunks:
-                if ("at", c, h) not in made:
-                    made["at", c, h] = make_at(c, h, banks[RING])
-                if g == 0 and h == 0:
-                    in_ring("av", make_av, c, h)
-                    in_ring("tg", make_tg, c, h)
-                else:
-                    in_ring("tg", make_tg, c, h)
-                    in_ring("av", make_av, c, h)
-            diffs = [result("diff", c, h) for c in chunks]
             gated = [work.tile([P, HALF], F32, name="gated") for c in chunks]
             res = [work.tile([P, HALF], F32, name="res") for c in chunks]
-            for c, d in zip(chunks, diffs):
-                nc.vector.tensor_tensor(d[:], made["av", c, h][:], made["at", c, h][:], SUB)
-            for c, d, m in zip(chunks, diffs, gated):
-                nc.vector.scalar_tensor_tensor(m[:], made["tg", c, h][:], 1.0, d[:], ADD, MULT)
+            for c, m in zip(chunks, gated):
+                nc.vector.scalar_tensor_tensor(m[:], made["tg", c, h][:], 1.0, made["diff", c, h][:], ADD, MULT)
             for c, m, r in zip(chunks, gated, res):
                 nc.vector.scalar_tensor_tensor(r[:], m[:], 0.5, made["at", c, h][:], MULT, ADD)
-                made["res", c, h] = r
                 nc.sync.dma_start(out=out[c * P : (c + 1) * P, h * HALF : (h + 1) * HALF], in_=r[:])
 
-        for a in range(K_PASSES):
-            round_wv(1, a)
-        quantise_wv(1)
-        for g in range(WV_PARTS):
-            for h in range(HALVES):
-                blend(g, h)
+        products("av", make_av, 0, 0)
+        products("tg", make_tg, 0, 0)
+        differences(0, 0)
+        blend(0, 0)
+        round_wv(1, 0)
+        products("av", make_av, 0, 1)
+        round_wv(1, 1)
+        products("tg", make_tg, 0, 1)
+        differences(0, 1)
+        quantise_late()
+        blend(0, 1)
+        for h in range(HALVES):
+            products("av", make_av, 1, h)
+            products("tg", make_tg, 1, h)
+            differences(1, h)
+            blend(1, h)

@@ -24,14 +24,14 @@ QUADS, QUAD, ROWS = 4, 32, 4
 BLOCKS = QUADS * ROWS
 LAST_QUAD = QUAD * (QUADS - 1)
 HALF = 512
-RING = 4
-FIRST_MOVES = 1
-EARLY = 8
 HALVES = J // HALF
-LIST_COLS = HALF // 16
+QUARTER = HALF // 2
 WV_COLS = 256
 WV_PARTS = N // WV_COLS
 CHUNKS = WV_COLS // P
+RING = 4
+FIRST_MOVES = 3
+EARLY = 7
 
 
 def tile_list_gmu_tanh_none_kernel(
@@ -51,234 +51,239 @@ def tile_list_gmu_tanh_none_kernel(
         def reused(shape, dtype, name, offset):
             return reuse.tile(shape, dtype, name=name, align_bytes=64, offset=offset)
 
+        tile_bytes = 4 * HALF
+        raw_shape = [P, PACK, WV_COLS]
         list1 = held([P, J // 16], U16, "list1")
         list2 = held([P, J // 16], U16, "list2")
-        raw_shape = [P, PACK, WV_COLS]
         tab_w = held([P, T], U32, "tab_w")
         tab_s = held([P, T], U8, "tab_s")
-        z_s = held([P, 4 * N], U8, "z_s")
-        zt_w = held([P, 2 * N], U8, "zt_w")
-        zv_w = held([P, K_PASSES, N], U32, "zv_w")
         tab2_w = held([P, T], U32, "tab2_w")
-        wv_raw = [[held(raw_shape, F32, "wv_raw%d%d" % (g, a)) for a in range(K_PASSES)] for g in range(WV_PARTS)]
-        tile_bytes = 4 * HALF
-        wv_bf0 = held([P, K_PASSES, WV_COLS, PACK], BF16, "wv_bf0")
-        wv_bf1 = reused([P, K_PASSES, WV_COLS, PACK], BF16, "wv_bf1", 0)
-        wv_bf = [[t[:, a] for a in range(K_PASSES)] for t in (wv_bf0, wv_bf1)]
-        pairs = [held([P, HALF // 2], U32, "pairs%d" % i) for i in range(2)]
         tab2_s = held([P, T], U8, "tab2_s")
+        zv_w = held([P, K_PASSES, N], U32, "zv_w")
+        zt_w = held([P, 2 * N], U8, "zt_w")
         wt_w = held([P, 2 * N], U8, "wt_w")
-        wt_s = z_s[:, 3 * N :]
-        z_rows = held([BLOCKS, 4 * N], U8, "z_rows")
+        z_rows = held([2 * BLOCKS, 3 * N], U8, "z_rows")[BLOCKS:, :]
+        z_s = held([P, 3 * N], U8, "z_s")
+        zv_s = [z_s[:, a * N : (a + 1) * N] for a in range(K_PASSES)]
+        zt_s = z_s[:, 2 * N :]
+        wt_s = held([P, N], U8, "wt_s")
         bias = held([P, N // P], F32, "bias")
         half_bias = held([P, N // P], F32, "half_bias")
+        wv_raw = [[held(raw_shape, F32, "wv_raw%d%d" % (g, a)) for a in range(K_PASSES)] for g in range(WV_PARTS)]
+        wv_bf0 = held([P, K_PASSES, WV_COLS, PACK], BF16, "wv_bf0")
+        wv_w0 = held([P, K_PASSES, WV_COLS], U32, "wv_w0")
+        wv_s0 = held([P, K_PASSES, WV_COLS], U8, "wv_s0")
+        late_bf = [reused([P, K_PASSES, P, PACK], BF16, "late_bf%d" % cc, cc * tile_bytes) for cc in range(CHUNKS)]
+        late_w = [held([P, K_PASSES, P], U32, "late_w%d" % cc) for cc in range(CHUNKS)]
+        late_s = [held([P, K_PASSES, P], U8, "late_s%d" % cc) for cc in range(CHUNKS)]
+        wv_w = [wv_w0[:, :, cc * P : (cc + 1) * P] for cc in range(CHUNKS)] + [t[:] for t in late_w]
+        wv_s = [wv_s0[:, :, cc * P : (cc + 1) * P] for cc in range(CHUNKS)] + [t[:] for t in late_s]
+        pairs = [held([P, QUARTER], U32, "pairs%d" % i) for i in range(2)]
         v_rows = held([P, J], U8, "v_rows")
         v_s = [held([P, J], U8, "v_s%d" % a) for a in range(K_PASSES)]
-        wv_w = [held([P, K_PASSES * WV_COLS], U32, "wv_w%d" % g) for g in range(WV_PARTS)]
-        wv_s = [held([P, K_PASSES * WV_COLS], U8, "wv_s%d" % g) for g in range(WV_PARTS)]
         v_w = [held([P, K_PASSES, 2 * HALF], U8, "v_w%d" % h) for h in range(HALVES)]
-        v2_w = [held([P, HALF], U32, "v2_w0"), held([P, HALF], U32, "v2_w1")]
-        after_rounding = {
-            ("diff", 0, 0): reused([P, HALF], F32, "diff00", 0),
-            ("tg", 0, 0): reused([P, HALF], F32, "tg00", tile_bytes),
+        v2_w = [held([P, HALF], U32, "v2_w%d" % h) for h in range(HALVES)]
+        v2_s = held([P, J], U8, "v2_s")
+        banks = [psum.tile([P, HALF], F32, name="bank%d" % i) for i in range(2 * RING)]
+        placed = {
+            ("tg", 0): reused([P, HALF], F32, "tg0", 0),
+            ("av", 3): reused([P, HALF], F32, "av3", tile_bytes),
         }
 
-        def result(kind, c, h):
-            if (kind, c, h) in after_rounding:
-                return after_rounding[kind, c, h]
+        def result(kind, i):
+            if (kind, i) in placed:
+                return placed[kind, i]
             return work.tile([P, HALF], F32, name=kind)
 
-        v2_all = held([P, J], U8, "v2_all")
-        v2_s = [v2_all[:, h * HALF : (h + 1) * HALF] for h in range(HALVES)]
-        banks = [psum.tile([P, HALF], F32, name="bank%d" % i) for i in range(2 * RING)]
-        zv_s = [z_s[:, a * N : (a + 1) * N] for a in range(K_PASSES)]
-        zt_s = z_s[:, 2 * N : 3 * N]
+        def load_bytes(tile, source):
+            nc.sync.dma_start(out=tile.bitcast(I32), in_=source.bitcast(I32))
 
-        nc.vector.memset(tab_s[0:LAST_QUAD, :].bitcast(I32), 0)
-        nc.gpsimd.memset(tab2_s[:].bitcast(I32), 0)
-
-        def gather(dst, window, offsets):
-            nc.vector.tensor_copy(dst, window[:].indirect(offsets))
-
-        def load_plane(queue, tile, rows, quads=range(QUADS)):
-            for q in quads:
-                queue.dma_start(
-                    out=tile[QUAD * q : QUAD * q + ROWS, :].bitcast(I32),
-                    in_=rows[ROWS * q : ROWS * (q + 1), :].bitcast(I32),
-                )
+        def load_plane(tile, rows, places=range(ROWS)):
+            for r in places:
+                load_bytes(tile[r:P:QUAD, :], rows[r:BLOCKS:ROWS, :])
 
         def load_wv(g, a):
             rows = wv[a * K_PASS : (a + 1) * K_PASS, g * WV_COLS : (g + 1) * WV_COLS]
             nc.sync.dma_start(out=wv_raw[g][a][:], in_=rows.rearrange("(p j) n -> p j n", j=PACK))
 
-        def load_table(tile, words):
-            nc.sync.dma_start(out=tile[:].bitcast(I32), in_=words[0].rearrange("p t i -> p (t i)").bitcast(I32))
+        def deal_picture_rows(moves):
+            for a, r in moves:
+                first = LAST_QUAD + BLOCKS * a
+                load_plane(v_s[a], v_rows[first : first + BLOCKS, :], [r])
 
-        def half_list(lst, h):
-            return lst[:, h * LIST_COLS : (h + 1) * LIST_COLS]
+        def gather(dst, window, lst, first, count):
+            nc.vector.tensor_copy(dst, window[:].indirect(lst[:, first // 16 : (first + count) // 16]))
 
-        def round_wv(g, a):
+        def round_wv(rounded, raw):
             nc.scalar.copy(
-                out=wv_bf[g][a].rearrange("p (c i) t -> p c t i", i=PACK),
-                in_=wv_raw[g][a][:].rearrange("p t (c i) -> p c t i", i=PACK),
+                out=rounded.rearrange("p (c i) t -> p c t i", i=PACK), in_=raw.rearrange("p t (c i) -> p c t i", i=PACK)
             )
 
-        def quantise_first():
+        def quantise(words, scales, rounded):
             nc.vector.quantize_mx(
-                out=wv_w[0][:].bitcast(FP8X4), scales=wv_s[0][:], in_=wv_bf0[:].rearrange("p a n t -> p (a n t)")
+                out=words[:].rearrange("p a n -> p (a n)").bitcast(FP8X4),
+                scales=scales[:].rearrange("p a n -> p (a n)"),
+                in_=rounded[:].rearrange("p a n t -> p (a n t)"),
             )
 
-        def quantise_late():
-            nc.vector.quantize_mx(
-                out=wv_w[1][:].bitcast(FP8X4), scales=wv_s[1][:], in_=wv_bf1[:].rearrange("p a n t -> p (a n t)")
-            )
+        def round_late(cc):
+            for a in range(K_PASSES):
+                round_wv(late_bf[cc][:, a], wv_raw[1][a][:, :, cc * P : (cc + 1) * P])
 
-        def gather_text(h):
-            gather(v2_w[h][:], tab2_w, half_list(list2, h))
+        def quantise_late(cc):
+            quantise(late_w[cc], late_s[cc], late_bf[cc])
 
         def gather_picture(h):
             for i in range(2):
-                first = h * LIST_COLS + i * LIST_COLS // 2
-                gather(pairs[i][:], tab_w, list1[:, first : first + LIST_COLS // 2])
+                gather(pairs[i][:], tab_w, list1, h * HALF + i * QUARTER, QUARTER)
             for i in range(2):
                 nc.vector.tensor_copy(
-                    out=v_w[h][:].bitcast(U16)[:, :, i * HALF // 2 : (i + 1) * HALF // 2],
+                    out=v_w[h][:].bitcast(U16)[:, :, i * QUARTER : (i + 1) * QUARTER],
                     in_=pairs[i][:].bitcast(U16).rearrange("p (j d) -> p d j", d=K_PASSES),
                 )
 
-
-        def deal_picture_rows(moves):
-            for a, q in moves:
-                first = LAST_QUAD + BLOCKS * a + ROWS * q
-                nc.sync.dma_start(
-                    out=v_s[a][QUAD * q : QUAD * q + ROWS, :].bitcast(I32), in_=v_rows[first : first + ROWS, :].bitcast(I32)
-                )
+        nc.vector.memset(tab_s[0:LAST_QUAD, :].bitcast(I32), 0)
+        nc.gpsimd.memset(tab2_s[:].bitcast(I32), 0)
 
         nc.sync.dma_start(list1[:], offs)
-        nc.sync.dma_start(
-            out=tab_s[LAST_QUAD:, :].bitcast(I32), in_=tab_scales.rearrange("a r t -> (a r) t").bitcast(I32)
-        )
+        load_bytes(tab_s[LAST_QUAD:, :], tab_scales.rearrange("a r t -> (a r) t"))
         nc.sync.dma_start(list2[:], offs2)
-        nc.sync.dma_start(
-            out=z_rows[:, : 2 * N].rearrange("r (a n) -> r a n", a=K_PASSES).bitcast(I32),
-            in_=zv_scales.rearrange("a r n -> r a n").bitcast(I32),
-        )
-        nc.sync.dma_start(out=z_rows[:, 2 * N : 3 * N].bitcast(I32), in_=zt_scales[0].bitcast(I32))
-        nc.sync.dma_start(out=z_rows[:, 3 * N :].bitcast(I32), in_=wt_scales[0].bitcast(I32))
+        load_bytes(z_rows[:, : 2 * N].rearrange("r (a n) -> r a n", a=K_PASSES), zv_scales.rearrange("a r n -> r a n"))
+        load_bytes(z_rows[:, 2 * N :], zt_scales[0])
+        load_plane(wt_s, wt_scales[0], range(1))
         load_wv(0, 0)
-        nc.sync.dma_start(out=wt_w[:].bitcast(I32), in_=wt_words[0].bitcast(I32))
-        load_plane(nc.sync, tab2_s, tab2_scales[0])
-        load_table(tab2_w, tab2_words)
+        load_bytes(wt_w[:], wt_words[0])
+        load_plane(tab2_s, tab2_scales[0])
+        load_plane(wt_s, wt_scales[0], range(1, 2))
+        load_bytes(tab2_w[:], tab2_words[0].rearrange("p t i -> p (t i)"))
         load_wv(0, 1)
-        load_plane(nc.sync, z_s, z_rows)
-        gather(v_rows[:], tab_s, list1[:])
-        moves = [(a, q) for a in range(K_PASSES) for q in range(QUADS)]
+        load_plane(wt_s, wt_scales[0], range(2, ROWS))
+        gather(v_rows[:], tab_s, list1, 0, J)
+        moves = [(a, r) for a in range(K_PASSES) for r in range(ROWS)]
         deal_picture_rows(moves[:FIRST_MOVES])
-        load_table(tab_w, tab_words)
-        deal_picture_rows(moves[FIRST_MOVES:-1])
-        nc.sync.dma_start(out=zv_w[:].bitcast(I32), in_=zv_words.rearrange("a p n i -> p a (n i)").bitcast(I32))
-        deal_picture_rows(moves[-1:])
-        nc.sync.dma_start(out=zt_w[:].bitcast(I32), in_=zt_words[0].bitcast(I32))
+        load_bytes(tab_w[:], tab_words[0].rearrange("p t i -> p (t i)"))
+        deal_picture_rows(moves[FIRST_MOVES:])
+        load_bytes(zv_w[:], zv_words.rearrange("a p n i -> p a (n i)"))
+        load_bytes(zt_w[:], zt_words[0])
+        load_plane(z_s, z_rows)
         with nc.allow_non_contiguous_dma(reason="one bias value a partition"):
             nc.sync.dma_start(out=bias[:], in_=b.rearrange("(c p) -> p c", p=P))
-        load_wv(1, 0)
-        load_wv(1, 1)
-        round_wv(0, 0)
-        round_wv(0, 1)
-        gather(v2_all[:], tab2_s, list2[:])
-        gather_text(0)
-        gather_text(1)
-        quantise_first()
-        nc.scalar.mul(half_bias[:], bias[:], 0.5)
-        gather_picture(0)
-        gather_picture(1)
+        for a in range(K_PASSES):
+            load_wv(1, a)
+
+        for a in range(K_PASSES):
+            round_wv(wv_bf0[:, a], wv_raw[0][a][:])
+        gather(v2_s[:], tab2_s, list2, 0, J)
+        for h in range(HALVES):
+            gather(v2_w[h][:], tab2_w, list2, h * HALF, HALF)
+        quantise(wv_w0, wv_s0, wv_bf0)
+        for h in range(HALVES):
+            gather_picture(h)
+
+        tiles = [(cc, h) for h in range(HALVES) for cc in range(CHUNKS)]
+        tiles = tiles + [(CHUNKS + cc, h) for cc in range(CHUNKS) for h in range(HALVES)]
+        made = {}
 
         def text(h):
-            return dict(rhs=v2_w[h][:].bitcast(FP8X4), rhs_scale=v2_s[h])
+            return dict(rhs=v2_w[h][:].bitcast(FP8X4), rhs_scale=v2_s[:, h * HALF : (h + 1) * HALF])
 
         def picture(h, a):
             return dict(rhs=v_w[h][:, a, :].bitcast(FP4X4), rhs_scale=v_s[a][:, h * HALF : (h + 1) * HALF])
 
-        def make_at(c, h, bank):
+        def make_at(i, bank):
+            c, h = tiles[i]
             nc.tensor.matmul_mx(
                 out=bank[:], lhsT=wt_w[:, 2 * c * P : 2 * (c + 1) * P].bitcast(FP4X4), lhsT_scale=wt_s[:, c * P : (c + 1) * P],
                 start=True, stop=True, **text(h),
             )
-            at = result("at", c, h)
-            nc.scalar.activation(at[:], bank[:], TANH)
-            return at
+            made["at", i] = result("at", i)
+            nc.scalar.activation(made["at", i][:], bank[:], TANH)
 
-        def make_tg(c, h, bank):
+        def make_tg(i, bank):
+            c, h = tiles[i]
             cols = slice(c * P, (c + 1) * P)
             nc.tensor.matmul_mx(
                 out=bank[:], lhsT=zt_w[:, 2 * c * P : 2 * (c + 1) * P].bitcast(FP4X4), lhsT_scale=zt_s[:, cols],
                 start=True, stop=False, **text(h),
             )
-            for a in reversed(range(K_PASSES)):
+            for a in range(K_PASSES):
                 nc.tensor.matmul_mx(
                     out=bank[:], lhsT=zv_w[:, a, cols].bitcast(FP8X4), lhsT_scale=zv_s[a][:, cols],
-                    start=False, stop=(a == 0), **picture(h, a),
+                    start=False, stop=(a == K_PASSES - 1), **picture(h, a),
                 )
-            tg = result("tg", c, h)
-            nc.scalar.activation(tg[:], bank[:], TANH, bias=half_bias[:, c : c + 1], scale=0.5)
-            return tg
+            made["tg", i] = result("tg", i)
+            nc.scalar.activation(made["tg", i][:], bank[:], TANH, bias=half_bias[:, c : c + 1], scale=0.5)
 
-        def make_av(c, h, bank):
-            g, cc = divmod(c, CHUNKS)
+        def make_av(i, bank):
+            c, h = tiles[i]
             for a in reversed(range(K_PASSES)):
-                wcols = slice(a * WV_COLS + cc * P, a * WV_COLS + (cc + 1) * P)
                 nc.tensor.matmul_mx(
-                    out=bank[:], lhsT=wv_w[g][:, wcols].bitcast(FP8X4), lhsT_scale=wv_s[g][:, wcols],
+                    out=bank[:], lhsT=wv_w[c][:, a, :].bitcast(FP8X4), lhsT_scale=wv_s[c][:, a, :],
                     start=(a == K_PASSES - 1), stop=(a == 0), **picture(h, a),
                 )
-            av = result("av", c, h)
-            nc.scalar.activation(av[:], bank[:], TANH)
-            return av
+            made["av", i] = result("av", i)
+            nc.scalar.activation(made["av", i][:], bank[:], TANH)
 
-        tiles = [(c, h) for h in range(HALVES) for c in range(N // P)]
-        made = {}
-        for i, (c, h) in enumerate(tiles[:EARLY]):
-            made["at", c, h] = make_at(c, h, banks[RING + i % RING])
+        def differ(i):
+            made["diff", i] = result("diff", i)
+            nc.vector.tensor_tensor(made["diff", i][:], made["av", i][:], made["at", i][:], SUB)
 
-        turns = []
+        def gate(i, cols):
+            nc.vector.scalar_tensor_tensor(
+                made["gated", i][:, cols], made["tg", i][:, cols], 1.0, made["diff", i][:, cols], ADD, MULT
+            )
 
-        def in_ring(kind, maker, c, h):
-            pair, turn = divmod(len(turns), RING)
-            made[kind, c, h] = maker(c, h, banks[RING * (max(pair - 1, 0) % 2) + turn])
-            turns.append(kind)
+        def finish(i, cols):
+            c, h = tiles[i]
+            res = made["res", i][:, cols]
+            nc.vector.scalar_tensor_tensor(res, made["gated", i][:, cols], 0.5, made["at", i][:, cols], MULT, ADD)
+            nc.sync.dma_start(out=out[c * P : (c + 1) * P, h * HALF + cols.start : h * HALF + cols.stop], in_=res)
 
-        def products(kind, maker, g, h):
-            for c in range(g * CHUNKS, (g + 1) * CHUNKS):
-                in_ring(kind, maker, c, h)
+        early = sorted(range(EARLY), key=lambda i: tiles[i][1])
+        for turn, i in enumerate(early):
+            make_at(i, banks[RING + turn % RING])
+        nc.gpsimd.tensor_scalar(half_bias[:], bias[:], 0.5, 0.0, MULT, ADD)
 
-        def differences(g, h):
-            for c in range(g * CHUNKS, (g + 1) * CHUNKS):
-                made["diff", c, h] = result("diff", c, h)
-                nc.vector.tensor_tensor(made["diff", c, h][:], made["av", c, h][:], made["at", c, h][:], SUB)
+        def products(maker, pair, first_bank):
+            for cc in range(CHUNKS):
+                maker(pair * CHUNKS + cc, banks[first_bank + cc])
 
-        def blend(g, h):
-            chunks = range(g * CHUNKS, (g + 1) * CHUNKS)
-            gated = [work.tile([P, HALF], F32, name="gated") for c in chunks]
-            res = [work.tile([P, HALF], F32, name="res") for c in chunks]
-            for c, m in zip(chunks, gated):
-                nc.vector.scalar_tensor_tensor(m[:], made["tg", c, h][:], 1.0, made["diff", c, h][:], ADD, MULT)
-            for c, m, r in zip(chunks, gated, res):
-                nc.vector.scalar_tensor_tensor(r[:], m[:], 0.5, made["at", c, h][:], MULT, ADD)
-                nc.sync.dma_start(out=out[c * P : (c + 1) * P, h * HALF : (h + 1) * HALF], in_=r[:])
+        def differences(pair):
+            for i in range(pair * CHUNKS, (pair + 1) * CHUNKS):
+                differ(i)
+                made["gated", i], made["res", i] = result("gated", i), result("res", i)
 
-        products("av", make_av, 0, 0)
-        products("tg", make_tg, 0, 0)
-        differences(0, 0)
-        blend(0, 0)
-        round_wv(1, 0)
-        products("av", make_av, 0, 1)
-        round_wv(1, 1)
-        products("tg", make_tg, 0, 1)
-        differences(0, 1)
-        quantise_late()
-        blend(0, 1)
-        for h in range(HALVES):
-            products("av", make_av, 1, h)
-            products("tg", make_tg, 1, h)
-            differences(1, h)
-            blend(1, h)
+        def blend(pair):
+            for step in (gate, finish):
+                for i in range(pair * CHUNKS, (pair + 1) * CHUNKS):
+                    step(i, whole)
+
+        whole = slice(0, HALF)
+        products(make_av, 0, 0)
+        products(make_tg, 0, 2)
+        differences(0)
+        blend(0)
+        products(make_av, 1, 2)
+        round_late(0)
+        products(make_tg, 1, 0)
+        differences(1)
+        round_late(1)
+        quantise_late(0)
+        blend(1)
+        products(make_av, 2, 4)
+        products(make_tg, 2, 6)
+        differences(2)
+        quantise_late(1)
+        blend(2)
+        make_at(len(tiles) - 1, banks[4])
+        products(make_av, 3, 0)
+        products(make_tg, 3, 2)
+        differences(3)
+        last = len(tiles) - 1
+        left, right = slice(0, QUARTER), slice(QUARTER, HALF)
+        gate(last - 1, whole)
+        gate(last, left)
+        finish(last - 1, whole)
+        gate(last, right)
+        finish(last, left)
+        finish(last, right)

@@ -30,7 +30,7 @@ WV_COLS = 256
 WV_PARTS = N // WV_COLS
 CHUNKS = WV_COLS // P
 RING = 4
-FIRST_MOVES = 3
+FIRST_MOVES = 6
 EARLY = 7
 
 
@@ -69,7 +69,10 @@ def tile_list_gmu_tanh_none_kernel(
         wt_s = held([P, N], U8, "wt_s")
         bias = held([P, N // P], F32, "bias")
         half_bias = held([P, N // P], F32, "half_bias")
-        wv_raw = [[held(raw_shape, F32, "wv_raw%d%d" % (g, a)) for a in range(K_PASSES)] for g in range(WV_PARTS)]
+        wv_raw = [
+            [held(raw_shape, F32, "wv_raw00"), reused(raw_shape, F32, "wv_raw01", 5 * tile_bytes // 2)],
+            [held(raw_shape, F32, "wv_raw1%d" % a) for a in range(K_PASSES)],
+        ]
         wv_bf0 = held([P, K_PASSES, WV_COLS, PACK], BF16, "wv_bf0")
         wv_w0 = held([P, K_PASSES, WV_COLS], U32, "wv_w0")
         wv_s0 = held([P, K_PASSES, WV_COLS], U8, "wv_s0")
@@ -86,6 +89,9 @@ def tile_list_gmu_tanh_none_kernel(
         v2_s = held([P, J], U8, "v2_s")
         banks = [psum.tile([P, HALF], F32, name="bank%d" % i) for i in range(2 * RING)]
         placed = {
+            ("at", 0): reused([P, HALF], F32, "at0", 2 * tile_bytes),
+            ("at", 1): reused([P, HALF], F32, "at1", 3 * tile_bytes),
+            ("at", 4): reused([P, HALF], F32, "at4", 4 * tile_bytes),
             ("tg", 0): reused([P, HALF], F32, "tg0", 0),
             ("av", 3): reused([P, HALF], F32, "av3", tile_bytes),
         }
@@ -95,8 +101,8 @@ def tile_list_gmu_tanh_none_kernel(
                 return placed[kind, i]
             return work.tile([P, HALF], F32, name=kind)
 
-        def load_bytes(tile, source):
-            nc.sync.dma_start(out=tile.bitcast(I32), in_=source.bitcast(I32))
+        def load_bytes(tile, source, queue=nc.sync):
+            queue.dma_start(out=tile.bitcast(I32), in_=source.bitcast(I32))
 
         def load_plane(tile, rows, places=range(ROWS)):
             for r in places:
@@ -142,28 +148,28 @@ def tile_list_gmu_tanh_none_kernel(
                     in_=pairs[i][:].bitcast(U16).rearrange("p (j d) -> p d j", d=K_PASSES),
                 )
 
-        nc.vector.memset(tab_s[0:LAST_QUAD, :].bitcast(I32), 0)
-        nc.gpsimd.memset(tab2_s[:].bitcast(I32), 0)
+        nc.vector.memset(tab2_s[:].bitcast(I32), 0)
+        nc.gpsimd.memset(tab_s[0:LAST_QUAD, :].bitcast(I32), 0)
 
         nc.sync.dma_start(list1[:], offs)
         load_bytes(tab_s[LAST_QUAD:, :], tab_scales.rearrange("a r t -> (a r) t"))
         nc.sync.dma_start(list2[:], offs2)
-        load_bytes(z_rows[:, : 2 * N].rearrange("r (a n) -> r a n", a=K_PASSES), zv_scales.rearrange("a r n -> r a n"))
-        load_bytes(z_rows[:, 2 * N :], zt_scales[0])
-        load_plane(wt_s, wt_scales[0], range(1))
         load_wv(0, 0)
-        load_bytes(wt_w[:], wt_words[0])
         load_plane(tab2_s, tab2_scales[0])
-        load_plane(wt_s, wt_scales[0], range(1, 2))
         load_bytes(tab2_w[:], tab2_words[0].rearrange("p t i -> p (t i)"))
+        load_bytes(wt_w[:], wt_words[0])
+        load_plane(wt_s, wt_scales[0])
         load_wv(0, 1)
-        load_plane(wt_s, wt_scales[0], range(2, ROWS))
+        load_bytes(tab_w[:], tab_words[0].rearrange("p t i -> p (t i)"))
+        load_bytes(
+            z_rows[:, : 2 * N].rearrange("r (a n) -> r a n", a=K_PASSES), zv_scales.rearrange("a r n -> r a n"), nc.gpsimd
+        )
+        load_bytes(z_rows[:, 2 * N :], zt_scales[0], nc.gpsimd)
         gather(v_rows[:], tab_s, list1, 0, J)
         moves = [(a, r) for a in range(K_PASSES) for r in range(ROWS)]
         deal_picture_rows(moves[:FIRST_MOVES])
-        load_bytes(tab_w[:], tab_words[0].rearrange("p t i -> p (t i)"))
-        deal_picture_rows(moves[FIRST_MOVES:])
         load_bytes(zv_w[:], zv_words.rearrange("a p n i -> p a (n i)"))
+        deal_picture_rows(moves[FIRST_MOVES:])
         load_bytes(zt_w[:], zt_words[0])
         load_plane(z_s, z_rows)
         with nc.allow_non_contiguous_dma(reason="one bias value a partition"):
@@ -241,7 +247,7 @@ def tile_list_gmu_tanh_none_kernel(
 
         early = sorted(range(EARLY), key=lambda i: tiles[i][1])
         for turn, i in enumerate(early):
-            make_at(i, banks[RING + turn % RING])
+            make_at(i, banks[RING + turn % (RING - 1)])
         nc.gpsimd.tensor_scalar(half_bias[:], bias[:], 0.5, 0.0, MULT, ADD)
 
         def products(maker, pair, first_bank):

@@ -31,7 +31,7 @@ WV_PARTS = N // WV_COLS
 CHUNKS = WV_COLS // P
 RING = 4
 FIRST_MOVES = 6
-EARLY = 7
+EARLY = 8
 
 
 def tile_list_gmu_tanh_none_kernel(
@@ -58,7 +58,7 @@ def tile_list_gmu_tanh_none_kernel(
         tab_w = held([P, T], U32, "tab_w")
         tab_s = held([P, T], U8, "tab_s")
         tab2_w = held([P, T], U32, "tab2_w")
-        tab2_s = held([P, T], U8, "tab2_s")
+        tab2_s = reused([P, T], U8, "tab2_s", 5 * tile_bytes)
         zv_w = held([P, K_PASSES, N], U32, "zv_w")
         zt_w = held([P, 2 * N], U8, "zt_w")
         wt_w = held([P, 2 * N], U8, "wt_w")
@@ -85,7 +85,7 @@ def tile_list_gmu_tanh_none_kernel(
         v_rows = held([P, J], U8, "v_rows")
         v_s = [held([P, J], U8, "v_s%d" % a) for a in range(K_PASSES)]
         v_w = [held([P, K_PASSES, 2 * HALF], U8, "v_w%d" % h) for h in range(HALVES)]
-        v2_w = [held([P, HALF], U32, "v2_w%d" % h) for h in range(HALVES)]
+        v2_w = [held([P, HALF], U32, "v2_w0"), reused([P, HALF], U32, "v2_w1", 5 * tile_bytes)]
         v2_s = held([P, J], U8, "v2_s")
         banks = [psum.tile([P, HALF], F32, name="bank%d" % i) for i in range(2 * RING)]
         placed = {
@@ -108,9 +108,9 @@ def tile_list_gmu_tanh_none_kernel(
             for r in places:
                 load_bytes(tile[r:P:QUAD, :], rows[r:BLOCKS:ROWS, :])
 
-        def load_wv(g, a):
+        def load_wv(g, a, queue=nc.sync):
             rows = wv[a * K_PASS : (a + 1) * K_PASS, g * WV_COLS : (g + 1) * WV_COLS]
-            nc.sync.dma_start(out=wv_raw[g][a][:], in_=rows.rearrange("(p j) n -> p j n", j=PACK))
+            queue.dma_start(out=wv_raw[g][a][:], in_=rows.rearrange("(p j) n -> p j n", j=PACK))
 
         def deal_picture_rows(moves):
             for a, r in moves:
@@ -152,14 +152,14 @@ def tile_list_gmu_tanh_none_kernel(
         nc.gpsimd.memset(tab_s[0:LAST_QUAD, :].bitcast(I32), 0)
 
         nc.sync.dma_start(list1[:], offs)
-        load_bytes(tab_s[LAST_QUAD:, :], tab_scales.rearrange("a r t -> (a r) t"))
+        load_bytes(tab_s[LAST_QUAD:, :], tab_scales.rearrange("a r t -> (a r) t"), nc.scalar)
         nc.sync.dma_start(list2[:], offs2)
-        load_wv(0, 0)
+        load_bytes(tab2_w[:], tab2_words[0].rearrange("p t i -> p (t i)"), nc.scalar)
         load_plane(tab2_s, tab2_scales[0])
-        load_bytes(tab2_w[:], tab2_words[0].rearrange("p t i -> p (t i)"))
+        for a in range(K_PASSES):
+            load_wv(0, a)
         load_bytes(wt_w[:], wt_words[0])
         load_plane(wt_s, wt_scales[0])
-        load_wv(0, 1)
         load_bytes(tab_w[:], tab_words[0].rearrange("p t i -> p (t i)"))
         load_bytes(
             z_rows[:, : 2 * N].rearrange("r (a n) -> r a n", a=K_PASSES), zv_scales.rearrange("a r n -> r a n"), nc.gpsimd
@@ -179,9 +179,10 @@ def tile_list_gmu_tanh_none_kernel(
 
         for a in range(K_PASSES):
             round_wv(wv_bf0[:, a], wv_raw[0][a][:])
-        gather(v2_s[:], tab2_s, list2, 0, J)
+        gather(v2_w[0][:], tab2_w, list2, 0, HALF)
         for h in range(HALVES):
-            gather(v2_w[h][:], tab2_w, list2, h * HALF, HALF)
+            gather(v2_s[:, h * HALF : (h + 1) * HALF], tab2_s, list2, h * HALF, HALF)
+        gather(v2_w[1][:], tab2_w, list2, HALF, HALF)
         quantise(wv_w0, wv_s0, wv_bf0)
         for h in range(HALVES):
             gather_picture(h)
@@ -281,7 +282,6 @@ def tile_list_gmu_tanh_none_kernel(
         differences(2)
         quantise_late(1)
         blend(2)
-        make_at(len(tiles) - 1, banks[4])
         products(make_av, 3, 0)
         products(make_tg, 3, 2)
         differences(3)

@@ -108,9 +108,9 @@ def tile_list_gmu_tanh_none_kernel(
             for r in places:
                 load_bytes(tile[r:P:QUAD, :], rows[r:BLOCKS:ROWS, :])
 
-        def load_wv(g, a, queue=nc.sync):
+        def load_wv(g, a):
             rows = wv[a * K_PASS : (a + 1) * K_PASS, g * WV_COLS : (g + 1) * WV_COLS]
-            queue.dma_start(out=wv_raw[g][a][:], in_=rows.rearrange("(p j) n -> p j n", j=PACK))
+            nc.sync.dma_start(out=wv_raw[g][a][:], in_=rows.rearrange("(p j) n -> p j n", j=PACK))
 
         def deal_picture_rows(moves):
             for a, r in moves:
@@ -152,9 +152,9 @@ def tile_list_gmu_tanh_none_kernel(
         nc.gpsimd.memset(tab_s[0:LAST_QUAD, :].bitcast(I32), 0)
 
         nc.sync.dma_start(list1[:], offs)
-        load_bytes(tab_s[LAST_QUAD:, :], tab_scales.rearrange("a r t -> (a r) t"), nc.scalar)
+        load_bytes(tab_s[LAST_QUAD:, :], tab_scales.rearrange("a r t -> (a r) t"))
+        load_bytes(tab2_w[:], tab2_words[0].rearrange("p t i -> p (t i)"))
         nc.sync.dma_start(list2[:], offs2)
-        load_bytes(tab2_w[:], tab2_words[0].rearrange("p t i -> p (t i)"), nc.scalar)
         load_plane(tab2_s, tab2_scales[0])
         for a in range(K_PASSES):
             load_wv(0, a)
@@ -194,8 +194,11 @@ def tile_list_gmu_tanh_none_kernel(
         def text(h):
             return dict(rhs=v2_w[h][:].bitcast(FP8X4), rhs_scale=v2_s[:, h * HALF : (h + 1) * HALF])
 
-        def picture(h, a):
-            return dict(rhs=v_w[h][:, a, :].bitcast(FP4X4), rhs_scale=v_s[a][:, h * HALF : (h + 1) * HALF])
+        def picture(h, a, first=0, width=HALF):
+            return dict(
+                rhs=v_w[h][:, a, 2 * first : 2 * (first + width)].bitcast(FP4X4),
+                rhs_scale=v_s[a][:, h * HALF + first : h * HALF + first + width],
+            )
 
         def make_at(i, bank):
             c, h = tiles[i]
@@ -223,11 +226,14 @@ def tile_list_gmu_tanh_none_kernel(
 
         def make_av(i, bank):
             c, h = tiles[i]
-            for a in reversed(range(K_PASSES)):
-                nc.tensor.matmul_mx(
-                    out=bank[:], lhsT=wv_w[c][:, a, :].bitcast(FP8X4), lhsT_scale=wv_s[c][:, a, :],
-                    start=(a == K_PASSES - 1), stop=(a == 0), **picture(h, a),
-                )
+            width = QUARTER if i < CHUNKS else HALF
+            for first in range(0, HALF, width):
+                for a in reversed(range(K_PASSES)):
+                    nc.tensor.matmul_mx(
+                        out=bank[:, first : first + width], lhsT=wv_w[c][:, a, :].bitcast(FP8X4),
+                        lhsT_scale=wv_s[c][:, a, :], start=(a == K_PASSES - 1), stop=(a == 0),
+                        **picture(h, a, first, width),
+                    )
             made["av", i] = result("av", i)
             nc.scalar.activation(made["av", i][:], bank[:], TANH)
 

@@ -1,6 +1,7 @@
 from contextlib import ExitStack
 
 import concourse.mybir as mybir
+from concourse.masks import make_identity
 
 K, L, N, T, J = 1024, 512, 512, 2048, 1024
 FLOPS = 2 * J * N * (2 * K + 2 * L)
@@ -32,6 +33,7 @@ CHUNKS = WV_COLS // P
 RING = 4
 FIRST_MOVES = 6
 EARLY = 8
+TURNED = 6
 
 
 def tile_list_gmu_tanh_none_kernel(
@@ -249,12 +251,54 @@ def tile_list_gmu_tanh_none_kernel(
         def finish(i, cols):
             c, h = tiles[i]
             res = made["res", i][:, cols]
-            nc.vector.scalar_tensor_tensor(res, made["gated", i][:, cols], 0.5, made["at", i][:, cols], MULT, ADD)
+            if i >= TURNED:
+                nc.vector.scalar_tensor_tensor(res, made["gated", i][:, cols], 0.5, made["minus_at", i][:, cols], MULT, SUB)
+            else:
+                nc.vector.scalar_tensor_tensor(res, made["gated", i][:, cols], 0.5, made["at", i][:, cols], MULT, ADD)
             nc.sync.dma_start(out=out[c * P : (c + 1) * P, h * HALF + cols.start : h * HALF + cols.stop], in_=res)
+
+        blocks = [slice(j, j + P) for j in range(0, HALF, P)]
+
+        def make_at_turned(i, bank):
+            c, h = tiles[i]
+            for js in blocks:
+                nc.tensor.matmul_mx(
+                    out=bank[:, js], lhsT=v2_w[h][:, js].bitcast(FP8X4),
+                    lhsT_scale=v2_s[:, h * HALF + js.start : h * HALF + js.stop],
+                    rhs=wt_w[:, 2 * c * P : 2 * (c + 1) * P].bitcast(FP4X4), rhs_scale=wt_s[:, c * P : (c + 1) * P],
+                    start=True, stop=True,
+                )
+            made["at", i] = result("at", i)
+            nc.scalar.activation(made["at", i][:], bank[:], TANH, scale=-1.0)
+
+        def make_av_turned(i, bank):
+            c, h = tiles[i]
+            for js in blocks:
+                for a in range(K_PASSES):
+                    nc.tensor.matmul_mx(
+                        out=bank[:, js], lhsT=v_w[h][:, a, 2 * js.start : 2 * js.stop].bitcast(FP4X4),
+                        lhsT_scale=v_s[a][:, h * HALF + js.start : h * HALF + js.stop],
+                        rhs=wv_w[c][:, a, :].bitcast(FP8X4), rhs_scale=wv_s[c][:, a, :],
+                        start=(a == 0), stop=(a == K_PASSES - 1),
+                    )
+            made["av", i] = result("av", i)
+            nc.scalar.activation(made["av", i][:], bank[:], TANH)
+
+        def turn_back(i, kinds, bank):
+            steps = [(kind, js) for kind in kinds for js in blocks]
+            for n, (kind, js) in enumerate(steps):
+                nc.tensor.matmul(
+                    bank[:, js], lhsT=made[kind, i][:, js], rhs=identity[:], is_transpose=True,
+                    start=(n == 0), stop=(n == len(steps) - 1),
+                )
+            return bank
 
         early = sorted(range(EARLY), key=lambda i: tiles[i][1])
         for turn, i in enumerate(early):
-            make_at(i, banks[RING + turn % (RING - 1)])
+            maker = make_at_turned if i >= TURNED else make_at
+            maker(i, banks[RING + turn % (RING - 1)])
+        identity = held([P, P], F32, "identity")
+        make_identity(nc, identity[:])
         nc.gpsimd.tensor_scalar(half_bias[:], bias[:], 0.5, 0.0, MULT, ADD)
 
         def products(maker, pair, first_bank):
@@ -284,13 +328,17 @@ def tile_list_gmu_tanh_none_kernel(
         quantise_late(0)
         blend(1)
         products(make_av, 2, 4)
+        quantise_late(1)
         products(make_tg, 2, 6)
         differences(2)
-        quantise_late(1)
-        blend(2)
-        products(make_av, 3, 0)
+        products(make_av_turned, 3, 0)
         products(make_tg, 3, 2)
-        differences(3)
+        blend(2)
+        for i in range(TURNED, len(tiles)):
+            made["diff", i] = turn_back(i, ("at", "av"), banks[RING + i - TURNED])
+            made["gated", i], made["res", i] = result("gated", i), result("res", i)
+        for i in range(TURNED, len(tiles)):
+            made["minus_at", i] = turn_back(i, ("at",), banks[RING + CHUNKS + i - TURNED])
         last = len(tiles) - 1
         left, right = slice(0, QUARTER), slice(QUARTER, HALF)
         gate(last - 1, whole)

@@ -21,18 +21,19 @@ P = 128
 PACK = 4
 K_PASS = P * PACK
 K_PASSES = K // K_PASS
-QUADS, QUAD, ROWS = 4, 32, 4
-BLOCKS = QUADS * ROWS
-LAST_QUAD = QUAD * (QUADS - 1)
+QUAD = 32
+ROWS = 4
+BLOCKS = K_PASS // 32
+LAST_QUAD = P - QUAD
+LIST_ROWS = 16
 HALF = 512
 HALVES = J // HALF
 QUARTER = HALF // 2
 WV_COLS = 256
-WV_PARTS = N // WV_COLS
 CHUNKS = WV_COLS // P
-RING = 4
+BANKS = 8
+EARLY_BANK, EARLY_BANKS = 4, 3
 FIRST_MOVES = 6
-EARLY = 8
 TURNED = 6
 
 
@@ -43,7 +44,7 @@ def tile_list_gmu_tanh_none_kernel(
     nc = tc.nc
     with ExitStack() as ctx:
         keep = ctx.enter_context(tc.tile_pool(name="keep", bufs=1))
-        work = ctx.enter_context(tc.tile_pool(name="work", bufs=8))
+        work = ctx.enter_context(tc.tile_pool(name="work", bufs=N // P * HALVES))
         reuse = ctx.enter_context(tc.tile_pool(name="reuse", bufs=1))
         psum = ctx.enter_context(tc.psum_pool(name="psum", bufs=1))
 
@@ -53,49 +54,49 @@ def tile_list_gmu_tanh_none_kernel(
         def reused(shape, dtype, name, offset):
             return reuse.tile(shape, dtype, name=name, align_bytes=64, offset=offset)
 
-        tile_bytes = 4 * HALF
+        unit = 4 * HALF
         raw_shape = [P, PACK, WV_COLS]
-        list1 = held([P, J // 16], U16, "list1")
-        list2 = held([P, J // 16], U16, "list2")
+        list1 = held([P, J // LIST_ROWS], U16, "list1")
+        list2 = held([P, J // LIST_ROWS], U16, "list2")
         tab_w = held([P, T], U32, "tab_w")
         tab_s = held([P, T], U8, "tab_s")
         tab2_w = held([P, T], U32, "tab2_w")
-        tab2_s = reused([P, T], U8, "tab2_s", 5 * tile_bytes)
+        tab2_s = reused([P, T], U8, "tab2_s", 5 * unit)
         zv_w = held([P, K_PASSES, N], U32, "zv_w")
         zt_w = held([P, 2 * N], U8, "zt_w")
         wt_w = held([P, 2 * N], U8, "wt_w")
         z_rows = held([2 * BLOCKS, 3 * N], U8, "z_rows")[BLOCKS:, :]
         z_s = held([P, 3 * N], U8, "z_s")
         zv_s = [z_s[:, a * N : (a + 1) * N] for a in range(K_PASSES)]
-        zt_s = z_s[:, 2 * N :]
+        zt_s = z_s[:, K_PASSES * N :]
         wt_s = held([P, N], U8, "wt_s")
         bias = held([P, N // P], F32, "bias")
         half_bias = held([P, N // P], F32, "half_bias")
         wv_raw = [
-            [held(raw_shape, F32, "wv_raw00"), reused(raw_shape, F32, "wv_raw01", 5 * tile_bytes // 2)],
+            [held(raw_shape, F32, "wv_raw00"), reused(raw_shape, F32, "wv_raw01", 5 * unit // 2)],
             [held(raw_shape, F32, "wv_raw1%d" % a) for a in range(K_PASSES)],
         ]
-        wv_bf0 = held([P, K_PASSES, WV_COLS, PACK], BF16, "wv_bf0")
-        wv_w0 = held([P, K_PASSES, WV_COLS], U32, "wv_w0")
-        wv_s0 = held([P, K_PASSES, WV_COLS], U8, "wv_s0")
-        late_bf = [reused([P, K_PASSES, P, PACK], BF16, "late_bf%d" % cc, cc * tile_bytes) for cc in range(CHUNKS)]
+        first_bf = held([P, K_PASSES, WV_COLS, PACK], BF16, "first_bf")
+        first_w = held([P, K_PASSES, WV_COLS], U32, "first_w")
+        first_s = held([P, K_PASSES, WV_COLS], U8, "first_s")
+        late_bf = [reused([P, K_PASSES, P, PACK], BF16, "late_bf%d" % cc, cc * unit) for cc in range(CHUNKS)]
         late_w = [held([P, K_PASSES, P], U32, "late_w%d" % cc) for cc in range(CHUNKS)]
         late_s = [held([P, K_PASSES, P], U8, "late_s%d" % cc) for cc in range(CHUNKS)]
-        wv_w = [wv_w0[:, :, cc * P : (cc + 1) * P] for cc in range(CHUNKS)] + [t[:] for t in late_w]
-        wv_s = [wv_s0[:, :, cc * P : (cc + 1) * P] for cc in range(CHUNKS)] + [t[:] for t in late_s]
-        pairs = [held([P, QUARTER], U32, "pairs%d" % i) for i in range(2)]
+        wv_w = [first_w[:, :, cc * P : (cc + 1) * P] for cc in range(CHUNKS)] + [t[:] for t in late_w]
+        wv_s = [first_s[:, :, cc * P : (cc + 1) * P] for cc in range(CHUNKS)] + [t[:] for t in late_s]
+        joined = [held([P, QUARTER], U32, "joined%d" % i) for i in range(2)]
         v_rows = held([P, J], U8, "v_rows")
         v_s = [held([P, J], U8, "v_s%d" % a) for a in range(K_PASSES)]
         v_w = [held([P, K_PASSES, 2 * HALF], U8, "v_w%d" % h) for h in range(HALVES)]
-        v2_w = [held([P, HALF], U32, "v2_w0"), reused([P, HALF], U32, "v2_w1", 5 * tile_bytes)]
+        v2_w = [held([P, HALF], U32, "v2_w0"), reused([P, HALF], U32, "v2_w1", 5 * unit)]
         v2_s = held([P, J], U8, "v2_s")
-        banks = [psum.tile([P, HALF], F32, name="bank%d" % i) for i in range(2 * RING)]
+        banks = [psum.tile([P, HALF], F32, name="bank%d" % i) for i in range(BANKS)]
         placed = {
-            ("at", 0): reused([P, HALF], F32, "at0", 2 * tile_bytes),
-            ("at", 1): reused([P, HALF], F32, "at1", 3 * tile_bytes),
-            ("at", 4): reused([P, HALF], F32, "at4", 4 * tile_bytes),
+            ("at", 0): reused([P, HALF], F32, "at0", 2 * unit),
+            ("at", 1): reused([P, HALF], F32, "at1", 3 * unit),
+            ("at", 4): reused([P, HALF], F32, "at4", 4 * unit),
             ("tg", 0): reused([P, HALF], F32, "tg0", 0),
-            ("av", 3): reused([P, HALF], F32, "av3", tile_bytes),
+            ("av", 3): reused([P, HALF], F32, "av3", unit),
         }
 
         def result(kind, i):
@@ -103,12 +104,12 @@ def tile_list_gmu_tanh_none_kernel(
                 return placed[kind, i]
             return work.tile([P, HALF], F32, name=kind)
 
-        def load_bytes(tile, source, queue=nc.sync):
+        def move_bytes(tile, source, queue=nc.sync):
             queue.dma_start(out=tile.bitcast(I32), in_=source.bitcast(I32))
 
-        def load_plane(tile, rows, places=range(ROWS)):
+        def fill_plane(plane, rows, places=range(ROWS)):
             for r in places:
-                load_bytes(tile[r:P:QUAD, :], rows[r:BLOCKS:ROWS, :])
+                move_bytes(plane[r:P:QUAD, :], rows[r:BLOCKS:ROWS, :])
 
         def load_wv(g, a):
             rows = wv[a * K_PASS : (a + 1) * K_PASS, g * WV_COLS : (g + 1) * WV_COLS]
@@ -117,14 +118,14 @@ def tile_list_gmu_tanh_none_kernel(
         def deal_picture_rows(moves):
             for a, r in moves:
                 first = LAST_QUAD + BLOCKS * a
-                load_plane(v_s[a], v_rows[first : first + BLOCKS, :], [r])
+                fill_plane(v_s[a], v_rows[first : first + BLOCKS, :], [r])
 
         def gather(dst, window, lst, first, count):
-            nc.vector.tensor_copy(dst, window[:].indirect(lst[:, first // 16 : (first + count) // 16]))
+            nc.vector.tensor_copy(dst, window[:].indirect(lst[:, first // LIST_ROWS : (first + count) // LIST_ROWS]))
 
         def round_wv(rounded, raw):
             nc.scalar.copy(
-                out=rounded.rearrange("p (c i) t -> p c t i", i=PACK), in_=raw.rearrange("p t (c i) -> p c t i", i=PACK)
+                out=rounded.rearrange("p (m i) t -> p m t i", i=PACK), in_=raw.rearrange("p t (m i) -> p m t i", i=PACK)
             )
 
         def quantise(words, scales, rounded):
@@ -143,179 +144,157 @@ def tile_list_gmu_tanh_none_kernel(
 
         def gather_picture(h):
             for i in range(2):
-                gather(pairs[i][:], tab_w, list1, h * HALF + i * QUARTER, QUARTER)
+                gather(joined[i][:], tab_w, list1, h * HALF + i * QUARTER, QUARTER)
             for i in range(2):
                 nc.vector.tensor_copy(
                     out=v_w[h][:].bitcast(U16)[:, :, i * QUARTER : (i + 1) * QUARTER],
-                    in_=pairs[i][:].bitcast(U16).rearrange("p (j d) -> p d j", d=K_PASSES),
+                    in_=joined[i][:].bitcast(U16).rearrange("p (j d) -> p d j", d=K_PASSES),
                 )
 
         nc.vector.memset(tab2_s[:].bitcast(I32), 0)
         nc.gpsimd.memset(tab_s[0:LAST_QUAD, :].bitcast(I32), 0)
 
         nc.sync.dma_start(list1[:], offs)
-        load_bytes(tab_s[LAST_QUAD:, :], tab_scales.rearrange("a r t -> (a r) t"))
-        load_bytes(tab2_w[:], tab2_words[0].rearrange("p t i -> p (t i)"))
+        move_bytes(tab_s[LAST_QUAD:, :], tab_scales.rearrange("a r t -> (a r) t"))
+        move_bytes(tab2_w[:], tab2_words[0].rearrange("p t i -> p (t i)"))
         nc.sync.dma_start(list2[:], offs2)
-        load_plane(tab2_s, tab2_scales[0])
+        fill_plane(tab2_s, tab2_scales[0])
         for a in range(K_PASSES):
             load_wv(0, a)
-        load_bytes(wt_w[:], wt_words[0])
-        load_plane(wt_s, wt_scales[0])
-        load_bytes(tab_w[:], tab_words[0].rearrange("p t i -> p (t i)"))
-        load_bytes(
-            z_rows[:, : 2 * N].rearrange("r (a n) -> r a n", a=K_PASSES), zv_scales.rearrange("a r n -> r a n"), nc.gpsimd
+        move_bytes(wt_w[:], wt_words[0])
+        fill_plane(wt_s, wt_scales[0])
+        move_bytes(tab_w[:], tab_words[0].rearrange("p t i -> p (t i)"))
+        move_bytes(
+            z_rows[:, : K_PASSES * N].rearrange("r (a n) -> r a n", a=K_PASSES),
+            zv_scales.rearrange("a r n -> r a n"),
+            nc.gpsimd,
         )
-        load_bytes(z_rows[:, 2 * N :], zt_scales[0], nc.gpsimd)
+        move_bytes(z_rows[:, K_PASSES * N :], zt_scales[0], nc.gpsimd)
         gather(v_rows[:], tab_s, list1, 0, J)
         moves = [(a, r) for a in range(K_PASSES) for r in range(ROWS)]
         deal_picture_rows(moves[:FIRST_MOVES])
-        load_bytes(zv_w[:], zv_words.rearrange("a p n i -> p a (n i)"))
+        move_bytes(zv_w[:], zv_words.rearrange("a p n i -> p a (n i)"))
         deal_picture_rows(moves[FIRST_MOVES:])
-        load_bytes(zt_w[:], zt_words[0])
-        load_plane(z_s, z_rows)
+        move_bytes(zt_w[:], zt_words[0])
+        fill_plane(z_s, z_rows)
         with nc.allow_non_contiguous_dma(reason="one bias value a partition"):
             nc.sync.dma_start(out=bias[:], in_=b.rearrange("(c p) -> p c", p=P))
         for a in range(K_PASSES):
             load_wv(1, a)
 
         for a in range(K_PASSES):
-            round_wv(wv_bf0[:, a], wv_raw[0][a][:])
+            round_wv(first_bf[:, a], wv_raw[0][a][:])
         gather(v2_w[0][:], tab2_w, list2, 0, HALF)
         for h in range(HALVES):
             gather(v2_s[:, h * HALF : (h + 1) * HALF], tab2_s, list2, h * HALF, HALF)
         gather(v2_w[1][:], tab2_w, list2, HALF, HALF)
-        quantise(wv_w0, wv_s0, wv_bf0)
+        quantise(first_w, first_s, first_bf)
         for h in range(HALVES):
             gather_picture(h)
 
         tiles = [(cc, h) for h in range(HALVES) for cc in range(CHUNKS)]
         tiles = tiles + [(CHUNKS + cc, h) for cc in range(CHUNKS) for h in range(HALVES)]
+        turned = range(TURNED, len(tiles))
+        blocks = [slice(j, j + P) for j in range(0, HALF, P)]
+        whole = slice(0, HALF)
         made = {}
 
-        def text(h):
-            return dict(rhs=v2_w[h][:].bitcast(FP8X4), rhs_scale=v2_s[:, h * HALF : (h + 1) * HALF])
+        def text(h, items=whole):
+            return v2_w[h][:, items].bitcast(FP8X4), v2_s[:, h * HALF + items.start : h * HALF + items.stop]
 
-        def picture(h, a, first=0, width=HALF):
-            return dict(
-                rhs=v_w[h][:, a, 2 * first : 2 * (first + width)].bitcast(FP4X4),
-                rhs_scale=v_s[a][:, h * HALF + first : h * HALF + first + width],
-            )
+        def picture(h, a, items=whole):
+            words = v_w[h][:, a, 2 * items.start : 2 * items.stop].bitcast(FP4X4)
+            return words, v_s[a][:, h * HALF + items.start : h * HALF + items.stop]
+
+        def fp4_weight(words, scales, c):
+            return words[:, 2 * c * P : 2 * (c + 1) * P].bitcast(FP4X4), scales[:, c * P : (c + 1) * P]
+
+        def wv_weight(c, a):
+            return wv_w[c][:, a, :].bitcast(FP8X4), wv_s[c][:, a, :]
+
+        def zv_weight(c, a):
+            return zv_w[:, a, c * P : (c + 1) * P].bitcast(FP8X4), zv_s[a][:, c * P : (c + 1) * P]
+
+        def add_up(sums, passes):
+            for n, (still, moving) in enumerate(passes):
+                nc.tensor.matmul_mx(
+                    out=sums, lhsT=still[0], lhsT_scale=still[1], rhs=moving[0], rhs_scale=moving[1],
+                    start=(n == 0), stop=(n == len(passes) - 1),
+                )
 
         def make_at(i, bank):
             c, h = tiles[i]
-            nc.tensor.matmul_mx(
-                out=bank[:], lhsT=wt_w[:, 2 * c * P : 2 * (c + 1) * P].bitcast(FP4X4), lhsT_scale=wt_s[:, c * P : (c + 1) * P],
-                start=True, stop=True, **text(h),
-            )
             made["at", i] = result("at", i)
-            nc.scalar.activation(made["at", i][:], bank[:], TANH)
-
-        def make_tg(i, bank):
-            c, h = tiles[i]
-            cols = slice(c * P, (c + 1) * P)
-            nc.tensor.matmul_mx(
-                out=bank[:], lhsT=zt_w[:, 2 * c * P : 2 * (c + 1) * P].bitcast(FP4X4), lhsT_scale=zt_s[:, cols],
-                start=True, stop=False, **text(h),
-            )
-            for a in range(K_PASSES):
-                nc.tensor.matmul_mx(
-                    out=bank[:], lhsT=zv_w[:, a, cols].bitcast(FP8X4), lhsT_scale=zv_s[a][:, cols],
-                    start=False, stop=(a == K_PASSES - 1), **picture(h, a),
-                )
-            made["tg", i] = result("tg", i)
-            nc.scalar.activation(made["tg", i][:], bank[:], TANH, bias=half_bias[:, c : c + 1], scale=0.5)
+            if i in turned:
+                for items in blocks:
+                    add_up(bank[:, items], [(text(h, items), fp4_weight(wt_w, wt_s, c))])
+                nc.scalar.activation(made["at", i][:], bank[:], TANH, scale=-1.0)
+            else:
+                add_up(bank[:], [(fp4_weight(wt_w, wt_s, c), text(h))])
+                nc.scalar.activation(made["at", i][:], bank[:], TANH)
 
         def make_av(i, bank):
             c, h = tiles[i]
-            width = QUARTER if i < CHUNKS else HALF
-            for first in range(0, HALF, width):
-                for a in reversed(range(K_PASSES)):
-                    nc.tensor.matmul_mx(
-                        out=bank[:, first : first + width], lhsT=wv_w[c][:, a, :].bitcast(FP8X4),
-                        lhsT_scale=wv_s[c][:, a, :], start=(a == K_PASSES - 1), stop=(a == 0),
-                        **picture(h, a, first, width),
-                    )
-            made["av", i] = result("av", i)
-            nc.scalar.activation(made["av", i][:], bank[:], TANH)
-
-        def differ(i):
-            made["diff", i] = result("diff", i)
-            nc.vector.tensor_tensor(made["diff", i][:], made["av", i][:], made["at", i][:], SUB)
-
-        def gate(i, cols):
-            nc.vector.scalar_tensor_tensor(
-                made["gated", i][:, cols], made["tg", i][:, cols], 1.0, made["diff", i][:, cols], ADD, MULT
-            )
-
-        def finish(i, cols):
-            c, h = tiles[i]
-            res = made["res", i][:, cols]
-            if i >= TURNED:
-                nc.vector.scalar_tensor_tensor(res, made["gated", i][:, cols], 0.5, made["minus_at", i][:, cols], MULT, SUB)
+            if i in turned:
+                for items in blocks:
+                    add_up(bank[:, items], [(picture(h, a, items), wv_weight(c, a)) for a in range(K_PASSES)])
             else:
-                nc.vector.scalar_tensor_tensor(res, made["gated", i][:, cols], 0.5, made["at", i][:, cols], MULT, ADD)
-            nc.sync.dma_start(out=out[c * P : (c + 1) * P, h * HALF + cols.start : h * HALF + cols.stop], in_=res)
-
-        blocks = [slice(j, j + P) for j in range(0, HALF, P)]
-
-        def make_at_turned(i, bank):
-            c, h = tiles[i]
-            for js in blocks:
-                nc.tensor.matmul_mx(
-                    out=bank[:, js], lhsT=v2_w[h][:, js].bitcast(FP8X4),
-                    lhsT_scale=v2_s[:, h * HALF + js.start : h * HALF + js.stop],
-                    rhs=wt_w[:, 2 * c * P : 2 * (c + 1) * P].bitcast(FP4X4), rhs_scale=wt_s[:, c * P : (c + 1) * P],
-                    start=True, stop=True,
-                )
-            made["at", i] = result("at", i)
-            nc.scalar.activation(made["at", i][:], bank[:], TANH, scale=-1.0)
-
-        def make_av_turned(i, bank):
-            c, h = tiles[i]
-            for js in blocks:
-                for a in range(K_PASSES):
-                    nc.tensor.matmul_mx(
-                        out=bank[:, js], lhsT=v_w[h][:, a, 2 * js.start : 2 * js.stop].bitcast(FP4X4),
-                        lhsT_scale=v_s[a][:, h * HALF + js.start : h * HALF + js.stop],
-                        rhs=wv_w[c][:, a, :].bitcast(FP8X4), rhs_scale=wv_s[c][:, a, :],
-                        start=(a == 0), stop=(a == K_PASSES - 1),
-                    )
+                width = QUARTER if i < CHUNKS else HALF
+                for items in [slice(j, j + width) for j in range(0, HALF, width)]:
+                    add_up(bank[:, items], [(wv_weight(c, a), picture(h, a, items)) for a in reversed(range(K_PASSES))])
             made["av", i] = result("av", i)
             nc.scalar.activation(made["av", i][:], bank[:], TANH)
+
+        def make_tg(i, bank):
+            c, h = tiles[i]
+            passes = [(fp4_weight(zt_w, zt_s, c), text(h))] + [(zv_weight(c, a), picture(h, a)) for a in range(K_PASSES)]
+            add_up(bank[:], passes)
+            made["tg", i] = result("tg", i)
+            nc.scalar.activation(made["tg", i][:], bank[:], TANH, bias=half_bias[:, c : c + 1], scale=0.5)
 
         def turn_back(i, kinds, bank):
-            steps = [(kind, js) for kind in kinds for js in blocks]
-            for n, (kind, js) in enumerate(steps):
+            steps = [(kind, items) for kind in kinds for items in blocks]
+            for n, (kind, items) in enumerate(steps):
                 nc.tensor.matmul(
-                    bank[:, js], lhsT=made[kind, i][:, js], rhs=identity[:], is_transpose=True,
+                    bank[:, items], lhsT=made[kind, i][:, items], rhs=identity[:], is_transpose=True,
                     start=(n == 0), stop=(n == len(steps) - 1),
                 )
             return bank
 
-        early = sorted(range(EARLY), key=lambda i: tiles[i][1])
-        for turn, i in enumerate(early):
-            maker = make_at_turned if i >= TURNED else make_at
-            maker(i, banks[RING + turn % (RING - 1)])
+        def gate(i):
+            nc.vector.scalar_tensor_tensor(made["gated", i][:], made["tg", i][:], 1.0, made["diff", i][:], ADD, MULT)
+
+        def finish(i, items=whole):
+            c, h = tiles[i]
+            term, op = (made["minus_at", i], SUB) if i in turned else (made["at", i], ADD)
+            res = made["res", i][:, items]
+            nc.vector.scalar_tensor_tensor(res, made["gated", i][:, items], 0.5, term[:, items], MULT, op)
+            nc.sync.dma_start(out=out[c * P : (c + 1) * P, h * HALF + items.start : h * HALF + items.stop], in_=res)
+
+        def pair(m):
+            return range(m * CHUNKS, (m + 1) * CHUNKS)
+
+        def products(maker, m, first_bank):
+            for cc, i in enumerate(pair(m)):
+                maker(i, banks[first_bank + cc])
+
+        def differences(m):
+            for i in pair(m):
+                made["diff", i] = result("diff", i)
+                nc.vector.tensor_tensor(made["diff", i][:], made["av", i][:], made["at", i][:], SUB)
+                made["gated", i], made["res", i] = result("gated", i), result("res", i)
+
+        def blend(m):
+            for step in (gate, finish):
+                for i in pair(m):
+                    step(i)
+
+        for turn, i in enumerate(sorted(range(len(tiles)), key=lambda i: tiles[i][1])):
+            make_at(i, banks[EARLY_BANK + turn % EARLY_BANKS])
         identity = held([P, P], F32, "identity")
         make_identity(nc, identity[:])
         nc.gpsimd.tensor_scalar(half_bias[:], bias[:], 0.5, 0.0, MULT, ADD)
 
-        def products(maker, pair, first_bank):
-            for cc in range(CHUNKS):
-                maker(pair * CHUNKS + cc, banks[first_bank + cc])
-
-        def differences(pair):
-            for i in range(pair * CHUNKS, (pair + 1) * CHUNKS):
-                differ(i)
-                made["gated", i], made["res", i] = result("gated", i), result("res", i)
-
-        def blend(pair):
-            for step in (gate, finish):
-                for i in range(pair * CHUNKS, (pair + 1) * CHUNKS):
-                    step(i, whole)
-
-        whole = slice(0, HALF)
         products(make_av, 0, 0)
         products(make_tg, 0, 2)
         differences(0)
@@ -331,19 +310,17 @@ def tile_list_gmu_tanh_none_kernel(
         quantise_late(1)
         products(make_tg, 2, 6)
         differences(2)
-        products(make_av_turned, 3, 0)
+        products(make_av, 3, 0)
         products(make_tg, 3, 2)
         blend(2)
-        for i in range(TURNED, len(tiles)):
-            made["diff", i] = turn_back(i, ("at", "av"), banks[RING + i - TURNED])
+
+        for cc, i in enumerate(turned):
+            made["diff", i] = turn_back(i, ("at", "av"), banks[4 + cc])
             made["gated", i], made["res", i] = result("gated", i), result("res", i)
-        for i in range(TURNED, len(tiles)):
-            made["minus_at", i] = turn_back(i, ("at",), banks[RING + CHUNKS + i - TURNED])
-        last = len(tiles) - 1
-        left, right = slice(0, QUARTER), slice(QUARTER, HALF)
-        gate(last - 1, whole)
-        gate(last, left)
-        finish(last - 1, whole)
-        gate(last, right)
-        finish(last, left)
-        finish(last, right)
+        for cc, i in enumerate(turned):
+            made["minus_at", i] = turn_back(i, ("at",), banks[6 + cc])
+        for i in turned:
+            gate(i)
+        for i in turned:
+            for first in range(0, HALF, QUARTER):
+                finish(i, slice(first, first + QUARTER))

@@ -61,7 +61,7 @@ def tile_list_gmu_tanh_none_kernel(
         tab_w = held([P, T], U32, "tab_w")
         tab_s = held([P, T], U8, "tab_s")
         tab2_w = held([P, T], U32, "tab2_w")
-        tab2_s = reused([P, T], U8, "tab2_s", 5 * unit)
+        tab2_s = reused([P, T], U8, "tab2_s", 2 * unit)
         zv_w = held([P, K_PASSES, N], U32, "zv_w")
         zt_w = held([P, 2 * N], U8, "zt_w")
         wt_w = held([P, 2 * N], U8, "wt_w")
@@ -73,7 +73,7 @@ def tile_list_gmu_tanh_none_kernel(
         bias = held([P, N // P], F32, "bias")
         half_bias = held([P, N // P], F32, "half_bias")
         wv_raw = [
-            [held(raw_shape, F32, "wv_raw00"), reused(raw_shape, F32, "wv_raw01", 5 * unit // 2)],
+            [held(raw_shape, F32, "wv_raw00"), held(raw_shape, F32, "wv_raw01")],
             [held(raw_shape, F32, "wv_raw1%d" % a) for a in range(K_PASSES)],
         ]
         first_bf = held([P, K_PASSES, WV_COLS, PACK], BF16, "first_bf")
@@ -88,13 +88,10 @@ def tile_list_gmu_tanh_none_kernel(
         v_rows = held([P, J], U8, "v_rows")
         v_s = [held([P, J], U8, "v_s%d" % a) for a in range(K_PASSES)]
         v_w = [held([P, K_PASSES, 2 * HALF], U8, "v_w%d" % h) for h in range(HALVES)]
-        v2_w = [held([P, HALF], U32, "v2_w0"), reused([P, HALF], U32, "v2_w1", 5 * unit)]
+        v2_w = [held([P, HALF], U32, "v2_w0"), reused([P, HALF], U32, "v2_w1", 2 * unit)]
         v2_s = held([P, J], U8, "v2_s")
         banks = [psum.tile([P, HALF], F32, name="bank%d" % i) for i in range(BANKS)]
         placed = {
-            ("at", 0): reused([P, HALF], F32, "at0", 2 * unit),
-            ("at", 1): reused([P, HALF], F32, "at1", 3 * unit),
-            ("at", 4): reused([P, HALF], F32, "at4", 4 * unit),
             ("tg", 0): reused([P, HALF], F32, "tg0", 0),
             ("av", 3): reused([P, HALF], F32, "av3", unit),
         }
@@ -182,8 +179,8 @@ def tile_list_gmu_tanh_none_kernel(
         for a in range(K_PASSES):
             load_wv(1, a)
 
-        for a in range(K_PASSES):
-            round_wv(first_bf[:, a], wv_raw[0][a][:])
+        round_wv(first_bf[:, 0], wv_raw[0][0][:])
+        nc.gpsimd.tensor_copy(out=first_bf[:, 1], in_=wv_raw[0][1][:].rearrange("p t n -> p n t"))
         gather(v2_w[0][:], tab2_w, list2, 0, HALF)
         for h in range(HALVES):
             gather(v2_s[:, h * HALF : (h + 1) * HALF], tab2_s, list2, h * HALF, HALF)
@@ -241,7 +238,7 @@ def tile_list_gmu_tanh_none_kernel(
             else:
                 width = QUARTER if i < CHUNKS else HALF
                 for items in [slice(j, j + width) for j in range(0, HALF, width)]:
-                    add_up(bank[:, items], [(wv_weight(c, a), picture(h, a, items)) for a in reversed(range(K_PASSES))])
+                    add_up(bank[:, items], [(wv_weight(c, a), picture(h, a, items)) for a in range(K_PASSES)])
             made["av", i] = result("av", i)
             nc.scalar.activation(made["av", i][:], bank[:], TANH)
 

@@ -35,6 +35,7 @@ BANKS = 8
 EARLY_BANK, EARLY_BANKS = 4, 3
 FIRST_MOVES = 6
 TURNED = 6
+HELPED = TURNED - 1
 
 
 def tile_list_gmu_tanh_none_kernel(
@@ -76,7 +77,7 @@ def tile_list_gmu_tanh_none_kernel(
             [held(raw_shape, F32, "wv_raw00"), held(raw_shape, F32, "wv_raw01")],
             [held(raw_shape, F32, "wv_raw1%d" % a) for a in range(K_PASSES)],
         ]
-        first_bf = held([P, K_PASSES, WV_COLS, PACK], BF16, "first_bf")
+        first_bf = reused([P, K_PASSES, WV_COLS, PACK], BF16, "first_bf", 3 * unit)
         first_w = held([P, K_PASSES, WV_COLS], U32, "first_w")
         first_s = held([P, K_PASSES, WV_COLS], U8, "first_s")
         late_bf = [reused([P, K_PASSES, P, PACK], BF16, "late_bf%d" % cc, cc * unit) for cc in range(CHUNKS)]
@@ -92,6 +93,7 @@ def tile_list_gmu_tanh_none_kernel(
         v2_s = held([P, J], U8, "v2_s")
         banks = [psum.tile([P, HALF], F32, name="bank%d" % i) for i in range(BANKS)]
         placed = {
+            ("half_at", HELPED): reused([P, HALF], F32, "half_at", 3 * unit),
             ("tg", 0): reused([P, HALF], F32, "tg0", 0),
             ("av", 3): reused([P, HALF], F32, "av3", unit),
         }
@@ -120,8 +122,8 @@ def tile_list_gmu_tanh_none_kernel(
         def gather(dst, window, lst, first, count):
             nc.vector.tensor_copy(dst, window[:].indirect(lst[:, first // LIST_ROWS : (first + count) // LIST_ROWS]))
 
-        def round_wv(rounded, raw):
-            nc.scalar.copy(
+        def round_wv(rounded, raw, copy=nc.scalar.copy):
+            copy(
                 out=rounded.rearrange("p (m i) t -> p m t i", i=PACK), in_=raw.rearrange("p t (m i) -> p m t i", i=PACK)
             )
 
@@ -132,9 +134,8 @@ def tile_list_gmu_tanh_none_kernel(
                 in_=rounded[:].rearrange("p a n t -> p (a n t)"),
             )
 
-        def round_late(cc):
-            for a in range(K_PASSES):
-                round_wv(late_bf[cc][:, a], wv_raw[1][a][:, :, cc * P : (cc + 1) * P])
+        def round_late(cc, a, copy=nc.scalar.copy):
+            round_wv(late_bf[cc][:, a], wv_raw[1][a][:, :, cc * P : (cc + 1) * P], copy)
 
         def quantise_late(cc):
             quantise(late_w[cc], late_s[cc], late_bf[cc])
@@ -190,7 +191,7 @@ def tile_list_gmu_tanh_none_kernel(
             gather_picture(h)
 
         tiles = [(cc, h) for h in range(HALVES) for cc in range(CHUNKS)]
-        tiles = tiles + [(CHUNKS + cc, h) for cc in range(CHUNKS) for h in range(HALVES)]
+        tiles = tiles + [(CHUNKS, h) for h in reversed(range(HALVES))] + [(CHUNKS + 1, h) for h in range(HALVES)]
         turned = range(TURNED, len(tiles))
         blocks = [slice(j, j + P) for j in range(0, HALF, P)]
         whole = slice(0, HALF)
@@ -265,7 +266,10 @@ def tile_list_gmu_tanh_none_kernel(
             c, h = tiles[i]
             term, op = (made["minus_at", i], SUB) if i in turned else (made["at", i], ADD)
             res = made["res", i][:, items]
-            nc.vector.scalar_tensor_tensor(res, made["gated", i][:, items], 0.5, term[:, items], MULT, op)
+            if i == HELPED:
+                nc.gpsimd.tensor_tensor(res, made["gated", i][:, items], term[:, items], ADD)
+            else:
+                nc.vector.scalar_tensor_tensor(res, made["gated", i][:, items], 0.5, term[:, items], MULT, op)
             nc.sync.dma_start(out=out[c * P : (c + 1) * P, h * HALF + items.start : h * HALF + items.stop], in_=res)
 
         def pair(m):
@@ -278,7 +282,11 @@ def tile_list_gmu_tanh_none_kernel(
         def differences(m):
             for i in pair(m):
                 made["diff", i] = result("diff", i)
-                nc.vector.tensor_tensor(made["diff", i][:], made["av", i][:], made["at", i][:], SUB)
+                if i == HELPED:
+                    half_at = made["half_at", i]
+                    nc.vector.scalar_tensor_tensor(made["diff", i][:], made["av", i][:], 0.5, half_at[:], MULT, SUB)
+                else:
+                    nc.vector.tensor_tensor(made["diff", i][:], made["av", i][:], made["at", i][:], SUB)
                 made["gated", i], made["res", i] = result("gated", i), result("res", i)
 
         def blend(m):
@@ -288,6 +296,8 @@ def tile_list_gmu_tanh_none_kernel(
 
         for turn, i in enumerate(sorted(range(len(tiles)), key=lambda i: tiles[i][1])):
             make_at(i, banks[EARLY_BANK + turn % EARLY_BANKS])
+        made["half_at", HELPED] = result("half_at", HELPED)
+        nc.gpsimd.tensor_scalar(made["half_at", HELPED][:], made["at", HELPED][:], 0.5, 0.0, MULT, ADD)
         identity = held([P, P], F32, "identity")
         make_identity(nc, identity[:])
         nc.gpsimd.tensor_scalar(half_bias[:], bias[:], 0.5, 0.0, MULT, ADD)
@@ -297,11 +307,13 @@ def tile_list_gmu_tanh_none_kernel(
         differences(0)
         blend(0)
         products(make_av, 1, 2)
-        round_late(0)
+        for a in range(K_PASSES):
+            round_late(0, a)
         products(make_tg, 1, 0)
         differences(1)
-        round_late(1)
+        round_late(1, 0)
         quantise_late(0)
+        round_late(1, 1, nc.vector.tensor_copy)
         blend(1)
         products(make_av, 2, 4)
         quantise_late(1)

@@ -32,7 +32,7 @@ QUARTER = HALF // 2
 WV_COLS = 256
 CHUNKS = WV_COLS // P
 BANKS = 8
-EARLY_BANK, EARLY_BANKS = 4, 3
+EARLY_BANK, EARLY_BANKS = 2, 6
 FIRST_MOVES = 6
 TURNED = 6
 HELPED = TURNED - 1

@@ -33,7 +33,7 @@ WV_COLS = 256
 CHUNKS = WV_COLS // P
 BANKS = 8
 EARLY_BANK, EARLY_BANKS = 2, 6
-FIRST_MOVES = 6
+FIRST_MOVES = 2
 TURNED = 6
 HELPED = TURNED - 1
 
@@ -150,7 +150,7 @@ def tile_list_gmu_tanh_none_kernel(
                 )
 
         nc.vector.memset(tab2_s[:].bitcast(I32), 0)
-        nc.gpsimd.memset(tab_s[0:LAST_QUAD, :].bitcast(I32), 0)
+        nc.vector.memset(tab_s[0:LAST_QUAD, :].bitcast(I32), 0)
 
         nc.sync.dma_start(list1[:], offs)
         move_bytes(tab_s[LAST_QUAD:, :], tab_scales.rearrange("a r t -> (a r) t"))
@@ -159,9 +159,8 @@ def tile_list_gmu_tanh_none_kernel(
         fill_plane(tab2_s, tab2_scales[0])
         for a in range(K_PASSES):
             load_wv(0, a)
-        move_bytes(wt_w[:], wt_words[0])
+        move_bytes(wt_w[:], wt_words[0], nc.gpsimd)
         fill_plane(wt_s, wt_scales[0])
-        move_bytes(tab_w[:], tab_words[0].rearrange("p t i -> p (t i)"))
         move_bytes(
             z_rows[:, : K_PASSES * N].rearrange("r (a n) -> r a n", a=K_PASSES),
             zv_scales.rearrange("a r n -> r a n"),
@@ -171,8 +170,9 @@ def tile_list_gmu_tanh_none_kernel(
         gather(v_rows[:], tab_s, list1, 0, J)
         moves = [(a, r) for a in range(K_PASSES) for r in range(ROWS)]
         deal_picture_rows(moves[:FIRST_MOVES])
-        move_bytes(zv_w[:], zv_words.rearrange("a p n i -> p a (n i)"))
+        move_bytes(tab_w[:], tab_words[0].rearrange("p t i -> p (t i)"))
         deal_picture_rows(moves[FIRST_MOVES:])
+        move_bytes(zv_w[:], zv_words.rearrange("a p n i -> p a (n i)"))
         move_bytes(zt_w[:], zt_words[0])
         fill_plane(z_s, z_rows)
         with nc.allow_non_contiguous_dma(reason="one bias value a partition"):

from contextlib import ExitStack

import concourse.mybir as mybir
from concourse.masks import make_identity

K, L, N, T, J = 1024, 512, 512, 2048, 1024
FLOPS = 2 * J * N * (2 * K + 2 * L)

F32 = mybir.dt.float32
BF16 = mybir.dt.bfloat16
I32 = mybir.dt.int32
U32 = mybir.dt.uint32
U16 = mybir.dt.uint16
U8 = mybir.dt.uint8
FP8X4 = mybir.dt.float8_e4m3fn_x4
FP4X4 = mybir.dt.float4_e2m1fn_x4
TANH = mybir.ActivationFunctionType.Tanh
ADD, SUB, MULT = mybir.AluOpType.add, mybir.AluOpType.subtract, mybir.AluOpType.mult

P = 128
PACK = 4
K_PASS = P * PACK
K_PASSES = K // K_PASS
QUAD = 32
ROWS = 4
BLOCKS = K_PASS // 32
LAST_QUAD = P - QUAD
LIST_ROWS = 16
HALF = 512
HALVES = J // HALF
QUARTER = HALF // 2
WV_COLS = 256
CHUNKS = WV_COLS // P
BANKS = 8
EARLY_BANK, EARLY_BANKS = 2, 6
FIRST_MOVES = 2
TURNED = 6
HELPED = TURNED - 1


def tile_list_gmu_tanh_none_kernel(
    tc, tab_words, tab_scales, tab2_words, tab2_scales, zv_words, zv_scales, zt_words, zt_scales,
    b, wv, wt_words, wt_scales, offs, offs2, out,
):
    nc = tc.nc
    with ExitStack() as ctx:
        keep = ctx.enter_context(tc.tile_pool(name="keep", bufs=1))
        work = ctx.enter_context(tc.tile_pool(name="work", bufs=N // P * HALVES))
        reuse = ctx.enter_context(tc.tile_pool(name="reuse", bufs=1))
        psum = ctx.enter_context(tc.psum_pool(name="psum", bufs=1))

        def held(shape, dtype, name):
            return keep.tile(shape, dtype, name=name, align_bytes=64)

        def reused(shape, dtype, name, offset):
            return reuse.tile(shape, dtype, name=name, align_bytes=64, offset=offset)

        unit = 4 * HALF
        raw_shape = [P, PACK, WV_COLS]
        list1 = held([P, J // LIST_ROWS], U16, "list1")
        list2 = held([P, J // LIST_ROWS], U16, "list2")
        tab_w = held([P, T], U32, "tab_w")
        tab_s = held([P, T], U8, "tab_s")
        tab2_w = held([P, T], U32, "tab2_w")
        tab2_s = reused([P, T], U8, "tab2_s", 2 * unit)
        zv_w = held([P, K_PASSES, N], U32, "zv_w")
        zt_w = held([P, 2 * N], U8, "zt_w")
        wt_w = held([P, 2 * N], U8, "wt_w")
        z_rows = held([2 * BLOCKS, 3 * N], U8, "z_rows")[BLOCKS:, :]
        z_s = held([P, 3 * N], U8, "z_s")
        zv_s = [z_s[:, a * N : (a + 1) * N] for a in range(K_PASSES)]
        zt_s = z_s[:, K_PASSES * N :]
        wt_s = held([P, N], U8, "wt_s")
        bias = held([P, N // P], F32, "bias")
        half_bias = held([P, N // P], F32, "half_bias")
        wv_raw = [
            [held(raw_shape, F32, "wv_raw00"), held(raw_shape, F32, "wv_raw01")],
            [held(raw_shape, F32, "wv_raw1%d" % a) for a in range(K_PASSES)],
        ]
        first_bf = reused([P, K_PASSES, WV_COLS, PACK], BF16, "first_bf", 3 * unit)
        first_w = held([P, K_PASSES, WV_COLS], U32, "first_w")
        first_s = held([P, K_PASSES, WV_COLS], U8, "first_s")
        late_bf = [reused([P, K_PASSES, P, PACK], BF16, "late_bf%d" % cc, cc * unit) for cc in range(CHUNKS)]
        late_w = [held([P, K_PASSES, P], U32, "late_w%d" % cc) for cc in range(CHUNKS)]
        late_s = [held([P, K_PASSES, P], U8, "late_s%d" % cc) for cc in range(CHUNKS)]
        wv_w = [first_w[:, :, cc * P : (cc + 1) * P] for cc in range(CHUNKS)] + [t[:] for t in late_w]
        wv_s = [first_s[:, :, cc * P : (cc + 1) * P] for cc in range(CHUNKS)] + [t[:] for t in late_s]
        joined = [held([P, QUARTER], U32, "joined%d" % i) for i in range(2)]
        v_rows = held([P, J], U8, "v_rows")
        v_s = [held([P, J], U8, "v_s%d" % a) for a in range(K_PASSES)]
        v_w = [held([P, K_PASSES, 2 * HALF], U8, "v_w%d" % h) for h in range(HALVES)]
        v2_w = [held([P, HALF], U32, "v2_w0"), reused([P, HALF], U32, "v2_w1", 2 * unit)]
        v2_s = held([P, J], U8, "v2_s")
        banks = [psum.tile([P, HALF], F32, name="bank%d" % i) for i in range(BANKS)]
        placed = {
            ("half_at", HELPED): reused([P, HALF], F32, "half_at", 3 * unit),
            ("tg", 0): reused([P, HALF], F32, "tg0", 0),
            ("av", 3): reused([P, HALF], F32, "av3", unit),
        }

        def result(kind, i):
            if (kind, i) in placed:
                return placed[kind, i]
            return work.tile([P, HALF], F32, name=kind)

        def move_bytes(tile, source, queue=nc.sync):
            queue.dma_start(out=tile.bitcast(I32), in_=source.bitcast(I32))

        def fill_plane(plane, rows, places=range(ROWS)):
            for r in places:
                move_bytes(plane[r:P:QUAD, :], rows[r:BLOCKS:ROWS, :])

        def load_wv(g, a):
            rows = wv[a * K_PASS : (a + 1) * K_PASS, g * WV_COLS : (g + 1) * WV_COLS]
            nc.sync.dma_start(out=wv_raw[g][a][:], in_=rows.rearrange("(p j) n -> p j n", j=PACK))

        def deal_picture_rows(moves):
            for a, r in moves:
                first = LAST_QUAD + BLOCKS * a
                fill_plane(v_s[a], v_rows[first : first + BLOCKS, :], [r])

        def gather(dst, window, lst, first, count):
            nc.vector.tensor_copy(dst, window[:].indirect(lst[:, first // LIST_ROWS : (first + count) // LIST_ROWS]))

        def round_wv(rounded, raw, copy=nc.scalar.copy):
            copy(
                out=rounded.rearrange("p (m i) t -> p m t i", i=PACK), in_=raw.rearrange("p t (m i) -> p m t i", i=PACK)
            )

        def quantise(words, scales, rounded):
            nc.vector.quantize_mx(
                out=words[:].rearrange("p a n -> p (a n)").bitcast(FP8X4),
                scales=scales[:].rearrange("p a n -> p (a n)"),
                in_=rounded[:].rearrange("p a n t -> p (a n t)"),
            )

        def round_late(cc, a, copy=nc.scalar.copy):
            round_wv(late_bf[cc][:, a], wv_raw[1][a][:, :, cc * P : (cc + 1) * P], copy)

        def quantise_late(cc):
            quantise(late_w[cc], late_s[cc], late_bf[cc])

        def gather_picture(h):
            for i in range(2):
                gather(joined[i][:], tab_w, list1, h * HALF + i * QUARTER, QUARTER)
            for i in range(2):
                nc.vector.tensor_copy(
                    out=v_w[h][:].bitcast(U16)[:, :, i * QUARTER : (i + 1) * QUARTER],
                    in_=joined[i][:].bitcast(U16).rearrange("p (j d) -> p d j", d=K_PASSES),
                )

        nc.vector.memset(tab2_s[:].bitcast(I32), 0)
        nc.vector.memset(tab_s[0:LAST_QUAD, :].bitcast(I32), 0)

        nc.sync.dma_start(list1[:], offs)
        move_bytes(tab_s[LAST_QUAD:, :], tab_scales.rearrange("a r t -> (a r) t"))
        move_bytes(tab2_w[:], tab2_words[0].rearrange("p t i -> p (t i)"))
        nc.sync.dma_start(list2[:], offs2)
        fill_plane(tab2_s, tab2_scales[0])
        for a in range(K_PASSES):
            load_wv(0, a)
        move_bytes(wt_w[:], wt_words[0], nc.gpsimd)
        fill_plane(wt_s, wt_scales[0])
        move_bytes(
            z_rows[:, : K_PASSES * N].rearrange("r (a n) -> r a n", a=K_PASSES),
            zv_scales.rearrange("a r n -> r a n"),
            nc.gpsimd,
        )
        move_bytes(z_rows[:, K_PASSES * N :], zt_scales[0], nc.gpsimd)
        gather(v_rows[:], tab_s, list1, 0, J)
        moves = [(a, r) for a in range(K_PASSES) for r in range(ROWS)]
        deal_picture_rows(moves[:FIRST_MOVES])
        move_bytes(tab_w[:], tab_words[0].rearrange("p t i -> p (t i)"))
        deal_picture_rows(moves[FIRST_MOVES:])
        move_bytes(zv_w[:], zv_words.rearrange("a p n i -> p a (n i)"))
        move_bytes(zt_w[:], zt_words[0])
        fill_plane(z_s, z_rows)
        with nc.allow_non_contiguous_dma(reason="one bias value a partition"):
            nc.sync.dma_start(out=bias[:], in_=b.rearrange("(c p) -> p c", p=P))
        for a in range(K_PASSES):
            load_wv(1, a)

        round_wv(first_bf[:, 0], wv_raw[0][0][:])
        nc.gpsimd.tensor_copy(out=first_bf[:, 1], in_=wv_raw[0][1][:].rearrange("p t n -> p n t"))
        gather(v2_w[0][:], tab2_w, list2, 0, HALF)
        for h in range(HALVES):
            gather(v2_s[:, h * HALF : (h + 1) * HALF], tab2_s, list2, h * HALF, HALF)
        gather(v2_w[1][:], tab2_w, list2, HALF, HALF)
        quantise(first_w, first_s, first_bf)
        for h in range(HALVES):
            gather_picture(h)

        tiles = [(cc, h) for h in range(HALVES) for cc in range(CHUNKS)]
        tiles = tiles + [(CHUNKS, h) for h in reversed(range(HALVES))] + [(CHUNKS + 1, h) for h in range(HALVES)]
        turned = range(TURNED, len(tiles))
        blocks = [slice(j, j + P) for j in range(0, HALF, P)]
        whole = slice(0, HALF)
        made = {}

        def text(h, items=whole):
            return v2_w[h][:, items].bitcast(FP8X4), v2_s[:, h * HALF + items.start : h * HALF + items.stop]

        def picture(h, a, items=whole):
            words = v_w[h][:, a, 2 * items.start : 2 * items.stop].bitcast(FP4X4)
            return words, v_s[a][:, h * HALF + items.start : h * HALF + items.stop]

        def fp4_weight(words, scales, c):
            return words[:, 2 * c * P : 2 * (c + 1) * P].bitcast(FP4X4), scales[:, c * P : (c + 1) * P]

        def wv_weight(c, a):
            return wv_w[c][:, a, :].bitcast(FP8X4), wv_s[c][:, a, :]

        def zv_weight(c, a):
            return zv_w[:, a, c * P : (c + 1) * P].bitcast(FP8X4), zv_s[a][:, c * P : (c + 1) * P]

        def add_up(sums, passes):
            for n, (still, moving) in enumerate(passes):
                nc.tensor.matmul_mx(
                    out=sums, lhsT=still[0], lhsT_scale=still[1], rhs=moving[0], rhs_scale=moving[1],
                    start=(n == 0), stop=(n == len(passes) - 1),
                )

        def make_at(i, bank):
            c, h = tiles[i]
            made["at", i] = result("at", i)
            if i in turned:
                for items in blocks:
                    add_up(bank[:, items], [(text(h, items), fp4_weight(wt_w, wt_s, c))])
                nc.scalar.activation(made["at", i][:], bank[:], TANH, scale=-1.0)
            else:
                add_up(bank[:], [(fp4_weight(wt_w, wt_s, c), text(h))])
                nc.scalar.activation(made["at", i][:], bank[:], TANH)

        def make_av(i, bank):
            c, h = tiles[i]
            if i in turned:
                for items in blocks:
                    add_up(bank[:, items], [(picture(h, a, items), wv_weight(c, a)) for a in range(K_PASSES)])
            else:
                width = QUARTER if i < CHUNKS else HALF
                for items in [slice(j, j + width) for j in range(0, HALF, width)]:
                    add_up(bank[:, items], [(wv_weight(c, a), picture(h, a, items)) for a in range(K_PASSES)])
            made["av", i] = result("av", i)
            nc.scalar.activation(made["av", i][:], bank[:], TANH)

        def make_tg(i, bank):
            c, h = tiles[i]
            passes = [(fp4_weight(zt_w, zt_s, c), text(h))] + [(zv_weight(c, a), picture(h, a)) for a in range(K_PASSES)]
            add_up(bank[:], passes)
            made["tg", i] = result("tg", i)
            nc.scalar.activation(made["tg", i][:], bank[:], TANH, bias=half_bias[:, c : c + 1], scale=0.5)

        def turn_back(i, kinds, bank):
            steps = [(kind, items) for kind in kinds for items in blocks]
            for n, (kind, items) in enumerate(steps):
                nc.tensor.matmul(
                    bank[:, items], lhsT=made[kind, i][:, items], rhs=identity[:], is_transpose=True,
                    start=(n == 0), stop=(n == len(steps) - 1),
                )
            return bank

        def gate(i):
            nc.vector.scalar_tensor_tensor(made["gated", i][:], made["tg", i][:], 1.0, made["diff", i][:], ADD, MULT)

        def finish(i, items=whole):
            c, h = tiles[i]
            term, op = (made["minus_at", i], SUB) if i in turned else (made["at", i], ADD)
            res = made["res", i][:, items]
            if i == HELPED:
                nc.gpsimd.tensor_tensor(res, made["gated", i][:, items], term[:, items], ADD)
            else:
                nc.vector.scalar_tensor_tensor(res, made["gated", i][:, items], 0.5, term[:, items], MULT, op)
            nc.sync.dma_start(out=out[c * P : (c + 1) * P, h * HALF + items.start : h * HALF + items.stop], in_=res)

        def pair(m):
            return range(m * CHUNKS, (m + 1) * CHUNKS)

        def products(maker, m, first_bank):
            for cc, i in enumerate(pair(m)):
                maker(i, banks[first_bank + cc])

        def differences(m):
            for i in pair(m):
                made["diff", i] = result("diff", i)
                if i == HELPED:
                    half_at = made["half_at", i]
                    nc.vector.scalar_tensor_tensor(made["diff", i][:], made["av", i][:], 0.5, half_at[:], MULT, SUB)
                else:
                    nc.vector.tensor_tensor(made["diff", i][:], made["av", i][:], made["at", i][:], SUB)
                made["gated", i], made["res", i] = result("gated", i), result("res", i)

        def blend(m):
            for step in (gate, finish):
                for i in pair(m):
                    step(i)

        for turn, i in enumerate(sorted(range(len(tiles)), key=lambda i: tiles[i][1])):
            make_at(i, banks[EARLY_BANK + turn % EARLY_BANKS])
        made["half_at", HELPED] = result("half_at", HELPED)
        nc.gpsimd.tensor_scalar(made["half_at", HELPED][:], made["at", HELPED][:], 0.5, 0.0, MULT, ADD)
        identity = held([P, P], F32, "identity")
        make_identity(nc, identity[:])
        nc.gpsimd.tensor_scalar(half_bias[:], bias[:], 0.5, 0.0, MULT, ADD)

        products(make_av, 0, 0)
        products(make_tg, 0, 2)
        differences(0)
        blend(0)
        products(make_av, 1, 2)
        for a in range(K_PASSES):
            round_late(0, a)
        products(make_tg, 1, 0)
        differences(1)
        round_late(1, 0)
        quantise_late(0)
        round_late(1, 1, nc.vector.tensor_copy)
        blend(1)
        products(make_av, 2, 4)
        quantise_late(1)
        products(make_tg, 2, 6)
        differences(2)
        products(make_av, 3, 0)
        products(make_tg, 3, 2)
        blend(2)

        for cc, i in enumerate(turned):
            made["diff", i] = turn_back(i, ("at", "av"), banks[4 + cc])
            made["gated", i], made["res", i] = result("gated", i), result("res", i)
        for cc, i in enumerate(turned):
            made["minus_at", i] = turn_back(i, ("at",), banks[6 + cc])
        for i in turned:
            gate(i)
        for i in turned:
            for first in range(0, HALF, QUARTER):
                finish(i, slice(first, first + QUARTER))
